import numpy as np
import ml_dtypes


def mxq(x, axis, fmt="e4m3"):
    dtype, down = {"e4m3": (ml_dtypes.float8_e4m3fn, 7), "e5m2": (ml_dtypes.float8_e5m2, 14)}[fmt]
    v = np.moveaxis(np.asarray(x, np.float32).astype(ml_dtypes.bfloat16).astype(np.float64), axis, -1)
    blocks = v.reshape(v.shape[:-1] + (-1, 32))
    amax = np.abs(blocks).max(-1, keepdims=True)
    byte = np.maximum(np.where(amax > 0, np.frexp(amax)[1] - 1 + 127, 0) - down, 1)
    scale = np.exp2(byte - 127.0)
    codes = (blocks / scale).astype(np.float32).astype(dtype).astype(np.float64)
    return np.moveaxis((codes * scale).reshape(v.shape), -1, axis)


WIDE = False


def mx_kscale(k):
    if not WIDE:
        return np.ones(k)
    levels = np.array([24, -24, 12, -12, 0])
    if k % 512:
        return np.exp2(np.random.permutation(np.resize(levels, k // 32))).repeat(32)
    a = np.empty((k // 512, 16))
    for p in range(k // 512):
        a[p, :8] = np.random.permutation(np.resize(levels, 8))
        for g in range(8):
            far = levels[np.abs(levels - a[p, g]) >= 10]
            a[p, g + 8] = far[np.random.randint(len(far))]
    return np.exp2(a.ravel()).repeat(32)


def f64(x):
    return np.asarray(x).astype(np.float64)


def striped8(idx):
    return np.concatenate([v.reshape(-1, 16).T for v in idx]).astype(np.uint16)


def unstriped8(offs):
    return np.stack([offs[16 * g:16 * g + 16].T.reshape(-1) for g in range(8)]).astype(np.int64)


E2M1 = np.array([0.0, 0.5, 1.0, 1.5, 2.0, 3.0, 4.0, 6.0, -0.0, -0.5, -1.0, -1.5, -2.0, -3.0, -4.0, -6.0])


def pack_weight(w, fmt):
    k, n = w.shape
    w = f64(np.asarray(w, np.float32).astype(ml_dtypes.bfloat16)).reshape(k // 32, 32, n)
    amax = np.abs(w).max(1)
    if fmt == "e4m3":
        byte = np.frexp(amax)[1] - 1 + 127 - 7
    else:
        mant, ex = np.frexp(amax / 6.0)
        byte = np.where(mant > 0.5, ex, ex - 1) + 127
    byte = np.clip(np.where(amax > 0, byte, 1), 1, 254)
    scaled = (w * np.exp2(127.0 - byte)[:, None, :]).reshape(k, n).astype(np.float32)
    by_word = np.ascontiguousarray(scaled.reshape(k // 512, 128, 4, n).transpose(0, 1, 3, 2))
    if fmt == "e4m3":
        words = by_word.astype(ml_dtypes.float8_e4m3fn).view(np.uint8)
    else:
        c = by_word.astype(ml_dtypes.float4_e2m1fn).view(np.uint8) & 0xF
        words = (c[..., 0::2] | (c[..., 1::2] << 4)).reshape(k // 512, 128, 2 * n)
    return np.ascontiguousarray(words), np.ascontiguousarray(byte.astype(np.uint8).reshape(k // 512, 16, n))


def unpack_weight(words, scales, fmt):
    g, _, n = scales.shape
    words = np.ascontiguousarray(words).reshape(g, 128, n, -1)
    if fmt == "e4m3":
        vals = words.view(ml_dtypes.float8_e4m3fn).astype(np.float64)
    else:
        nib = np.empty((g, 128, n, 4), np.uint8)
        nib[..., 0::2] = words & 0xF
        nib[..., 1::2] = words >> 4
        vals = E2M1[nib]
    vals = vals * np.repeat(np.exp2(scales.astype(np.float64) - 127.0), 8, axis=1)[..., None]
    return vals.transpose(0, 1, 3, 2).reshape(g * 512, n)


def planes(y):
    n, m = y.shape
    v = y.astype(np.float32).astype(ml_dtypes.bfloat16).astype(np.float64).reshape(n // 32, 32, m)
    top = np.abs(v).max(1)
    byte = np.clip(np.where(top > 0, np.frexp(top)[1] - 1 + 127 - 7, 1), 1, 254)
    codes = (v * np.exp2(127.0 - byte)[:, None, :]).reshape(n, m).astype(np.float32).astype(ml_dtypes.float8_e4m3fn).view(np.uint8)
    words = codes.reshape(n // 512, 128, 4, m).transpose(0, 1, 3, 2)
    return np.ascontiguousarray(words), np.ascontiguousarray(byte.astype(np.uint8).reshape(n // 512, 16, m))


K, L, N, T, J = 1024, 512, 512, 2048, 1024


def setup_inputs():
    n = np.random.standard_normal
    s = mx_kscale(K)[:, None]
    s2 = mx_kscale(L)[:, None]
    p_wt = pack_weight(n((K, N)) / np.sqrt(K) / s, "e2m1")
    p_wx = pack_weight(n((L, N)) / np.sqrt(L) / s2, "e4m3")
    return {
        "xT": (n((K, T)) * s).astype(np.float32),
        "wgt": np.repeat(np.random.uniform(0.5, 2.0, (8, J)), 16, axis=0).astype(np.float32),
        "wt_words": p_wt[0],
        "wt_scales": p_wt[1],
        "c": (n((L, J)) * s2).astype(np.float32),
        "wx_words": p_wx[0],
        "wx_scales": p_wx[1],
        "b": (0.3 * n(N)).astype(np.float32),
        "offs": striped8(np.stack([np.random.permutation(T)[:J] for _ in range(8)])),
    }


def reference(xT, wgt, wt_words, wt_scales, c, wx_words, wx_scales, b, offs):
    idx = unstriped8(offs)
    rows = np.arange(K)
    xg = f64(wgt)[rows // 4 % 128] * f64(xT)[rows[:, None], idx[rows % 512 // 64]]
    xT_ = mxq(xg, 0, "e4m3")
    wt_ = unpack_weight(wt_words, wt_scales, "e2m1")
    c_q_ = mxq(f64(c), 0, "e4m3")
    c_r_ = mxq(f64(c) - c_q_, 0, "e4m3")
    wx_ = unpack_weight(wx_words, wx_scales, "e4m3")
    y = wt_.T @ xT_ + wx_.T @ c_q_ + wx_.T @ c_r_
    out_0 = y + f64(b)[:, None]
    return (out_0,) + planes(out_0)

@@ -1,0 +1,327 @@
+from contextlib import ExitStack
+
+import concourse.mybir as mybir
+
+K, L, N, T, J = 1024, 512, 512, 2048, 1024
+FLOPS = 2 * N * J * (K + 2 * L) + 2 * L * L * J
+
+F32 = mybir.dt.float32
+BF16 = mybir.dt.bfloat16
+I32 = mybir.dt.int32
+U32 = mybir.dt.uint32
+U16 = mybir.dt.uint16
+U8 = mybir.dt.uint8
+FP8X4 = mybir.dt.float8_e4m3fn_x4
+FP4X4 = mybir.dt.float4_e2m1fn_x4
+ALU = mybir.AluOpType
+ACT = mybir.ActivationFunctionType
+
+P = 128
+PACK = 4
+BANK = 512
+W = 256
+QUARTERS = J // W
+SUB = 128
+WIDTHS = [256, 256, 256, 128, 128]
+STARTS = [sum(WIDTHS[:n]) for n in range(len(WIDTHS))]
+X_ROUND_ON_VECTOR = ()
+Y_ROUND_ON_VECTOR = (1, 2, 3, 4)
+KB = 1024
+
+
+def tile_list_biasP_kernel(
+    tc, xT, wgt, wt_words, wt_scales, c, wx_words, wx_scales, b, offs, out_0, out_1, out_2
+):
+    nc = tc.nc
+    with ExitStack() as ctx:
+        keep = ctx.enter_context(tc.tile_pool(name="keep", bufs=1))
+        shared = ctx.enter_context(tc.tile_pool(name="shared", bufs=1))
+        psum = ctx.enter_context(tc.psum_pool(name="psum", bufs=8))
+
+        def held(shape, dtype, name):
+            return keep.tile(shape, dtype, name=name, align_bytes=64)
+
+        def placed(shape, dtype, name, kib):
+            return shared.tile(shape, dtype, name=name, align_bytes=64, offset=kib * KB)
+
+        def planar(t3):
+            return t3.rearrange("p t (q i) -> p q t i", i=4)
+
+        def woven(t2):
+            return t2.rearrange("p (q i t) -> p q t i", i=4, t=PACK)
+
+        def weave(dst, src, on_vector):
+            if on_vector:
+                nc.vector.tensor_copy(out=woven(dst), in_=planar(src))
+            else:
+                nc.scalar.activation(out=woven(dst), in_=planar(src), func=ACT.Identity)
+
+        def quantize(src, name):
+            width = src.shape[1] // PACK
+            codes = held([P, width], U32, name + "_codes")
+            scales = held([P, width], U8, name + "_scales")
+            nc.vector.quantize_mx(out=codes[:].bitcast(FP8X4), scales=scales[:], in_=src)
+            return codes, scales
+
+        offsets = held([P, J // 16], U16, "offsets")
+        wt_raw = held([P, 2, 2 * N], U8, "wt_raw")
+        wx_raw = held([P, N], I32, "wx_raw")
+        sc_raw = held([P, 2, N], U8, "sc_raw")
+        bias = held([P, PACK], F32, "bias")
+        wgt_first = placed([P, WIDTHS[0]], F32, "wgt_first", 36)
+        wgt_rest = held([P, J - WIDTHS[0]], F32, "wgt_rest")
+        x_at = {1: 24}
+        x_sb = [
+            placed([P, T], F32, f"x{k}", x_at[k]) if k in x_at else held([P, T], F32, f"x{k}")
+            for k in range(2 * PACK)
+        ]
+        c_at = [0, 4, 16, 20]
+        c_sb = [placed([P, PACK, W], F32, f"c{h}", c_at[h]) for h in range(QUARTERS)]
+
+        nc.vector.memset(sc_raw[:].bitcast(I32), 0)
+        ones = held([P, P], F32, "ones")
+        ramp = held([P, P], F32, "ramp")
+        turned = held([P, P], F32, "turned")
+        eye = held([P, PACK * (L + 1)], BF16, "eye")
+        nc.vector.memset(ones[:], 1.0)
+        nc.vector.memset(eye[:].bitcast(I32), 0)
+        nc.vector.tensor_tensor_scan(out=ramp[:], data0=ones[:], data1=ones[:], initial=0.0, op0=ALU.mult, op1=ALU.add)
+        nc.vector.transpose(out=turned[:], in_=ramp[:])
+        eye_rows = eye[:].rearrange("p (t x) -> p t x", t=PACK)
+        for Q in range(4):
+            rows = slice(32 * Q, 32 * Q + 32)
+            nc.vector.tensor_tensor(
+                out=eye_rows[rows, :, P * Q : P * (Q + 1) : PACK],
+                in0=ramp[rows, :].rearrange("p (t m) -> p t m", t=PACK),
+                in1=turned[rows, :].rearrange("p (t m) -> p t m", t=PACK),
+                op=ALU.is_equal,
+            )
+        eye_codes, eye_scales = quantize(eye[:, 0 : PACK * L], "eye")
+
+        x_planes = xT.rearrange("(a p i) t -> a i p t", a=2, i=PACK)
+        c_rows = c.rearrange("(p t) j -> p t j", t=PACK)
+        wt_sc32 = wt_scales.bitcast(I32).rearrange("a q n -> q a n")
+        wx_sc32 = wx_scales.bitcast(I32)
+        sc32 = sc_raw[:].bitcast(I32)
+
+        small = []
+        for Q in range(4):
+            small.append((sc32[32 * Q : 32 * Q + 4, :, :], wt_sc32[4 * Q : 4 * Q + 4, :, :]))
+            small.append((sc32[32 * Q + 4 : 32 * Q + 8, 0, :], wx_sc32[0, 4 * Q : 4 * Q + 4, :]))
+
+        def load_x(k):
+            return (x_sb[k][:], x_planes[k // PACK, k % PACK])
+
+        def load_c(h):
+            return (c_sb[h][:], c_rows[:, :, h * W : (h + 1) * W])
+
+        loads = [
+            (wt_raw[:].bitcast(I32), wt_words.bitcast(I32).rearrange("a p n -> p a n")),
+            (wx_raw[:], wx_words[0].rearrange("p n i -> p (n i)").bitcast(I32)),
+            load_c(0),
+            load_c(1),
+            (offsets[:], offs),
+            (wgt_first[:], wgt[:, 0 : WIDTHS[0]]),
+            load_x(0),
+            (wgt_rest[:], wgt[:, WIDTHS[0] : J]),
+        ]
+        loads.extend(small[0:4] + [load_x(1)] + small[4:6] + [load_x(2)] + small[6:8] + [load_x(3)])
+        loads.extend([(bias[:], b.rearrange("(p t) -> p t", t=PACK)), load_c(2), load_c(3)])
+        loads.extend(load_x(k) for k in range(PACK, 2 * PACK))
+        for dst, src in loads:
+            nc.sync.dma_start(dst, src)
+
+        wt_d = held([P, 2 * 2 * N], U8, "wt_d")
+        nc.vector.tensor_copy(
+            out=wt_d[:].bitcast(U16).rearrange("p (a t m) -> p a t m", a=2, t=PACK),
+            in_=wt_raw[:].bitcast(U16).rearrange("p a (m t) -> p a t m", t=PACK),
+        )
+        wx_d = held([P, N], I32, "wx_d")
+        nc.vector.tensor_copy(
+            out=wx_d[:].rearrange("p (t q i) -> p q t i", t=PACK, i=4),
+            in_=wx_raw[:].rearrange("p (q i t) -> p q t i", t=PACK, i=4),
+        )
+
+        cb = {}
+        cq = {}
+        cr = {}
+        rb = {}
+
+        def round_c(h):
+            cb[h] = held([P, PACK * W], BF16, f"cb{h}") if h < 3 else placed([P, PACK * W], BF16, f"cb{h}", 40)
+            weave(cb[h][:], c_sb[h][:], False)
+
+        def first_tier(h):
+            cq[h] = quantize(cb[h][:], f"cq{h}")
+
+        def leftover(h):
+            codes, scales = cq[h]
+            rb[h] = held([P, PACK * W], BF16, f"rb{h}")
+            for s in range(W // SUB):
+                cols = slice(s * SUB, (s + 1) * SUB)
+                back = psum.tile([P, PACK, SUB], F32, name="back", tag="bank")
+                for t in range(PACK):
+                    nc.tensor.matmul_mx(
+                        out=back[:, t, :],
+                        lhsT=eye_codes[:, t * P : (t + 1) * P].bitcast(FP8X4),
+                        lhsT_scale=eye_scales[:, t * P : (t + 1) * P],
+                        rhs=codes[:, cols].bitcast(FP8X4),
+                        rhs_scale=scales[:, cols],
+                        start=True,
+                        stop=True,
+                    )
+                nc.vector.tensor_tensor(
+                    out=woven(rb[h][:, s * PACK * SUB : (s + 1) * PACK * SUB]),
+                    in0=planar(c_sb[h][:, :, cols]),
+                    in1=planar(back[:]),
+                    op=ALU.subtract,
+                )
+
+        def second_tier(h):
+            cr[h] = quantize(rb[h][:], f"cr{h}")
+
+        def gather(dst, k, j0, j1):
+            nc.vector.tensor_tensor(
+                out=dst,
+                in0=x_sb[k][:].indirect(offsets[:, j0 // 16 : j1 // 16]),
+                in1=wgt_first[:] if j0 == 0 else wgt_rest[:, j0 - WIDTHS[0] : j1 - WIDTHS[0]],
+                op=ALU.mult,
+            )
+
+        for h in range(2):
+            round_c(h)
+            first_tier(h)
+        for h in range(2):
+            leftover(h)
+        picked0 = placed([P, PACK, J], F32, "picked0", 0)
+        for i in range(PACK):
+            if i < 2:
+                second_tier(i)
+            gather(picked0[:, i, 0 : WIDTHS[0]], i, 0, WIDTHS[0])
+            gather(picked0[:, i, WIDTHS[0] : J], i, WIDTHS[0], J)
+            if i == 2:
+                sc_d = placed([P, 2 * N], U8, "sc_d", 24)
+                nc.vector.tensor_copy(
+                    out=sc_d[:].rearrange("p (a t m) -> p a t m", a=2, t=PACK),
+                    in_=sc_raw[:].rearrange("p a (m t) -> p a t m", t=PACK),
+                )
+        for h in range(2, QUARTERS):
+            round_c(h)
+            first_tier(h)
+        xb0 = placed([P, PACK * J], BF16, "xb0", 40)
+        for h in range(QUARTERS):
+            weave(xb0[:, h * PACK * W : (h + 1) * PACK * W], picked0[:, :, h * W : (h + 1) * W], False)
+        xq0 = {}
+
+        def quantize_first_pass(h):
+            xq0[h] = quantize(xb0[:, h * PACK * W : (h + 1) * PACK * W], f"xq0_{h}")
+
+        banks = {}
+
+        def sum_of(n, t):
+            per_bank = BANK // WIDTHS[n]
+            return banks[n, t // per_bank][:, t % per_bank, :]
+
+        def wx_pass(n, t, operand, cols, start):
+            codes, scales = operand
+            nc.tensor.matmul_mx(
+                out=sum_of(n, t),
+                lhsT=wx_d[:, t * P : (t + 1) * P].bitcast(FP8X4),
+                lhsT_scale=sc_d[4:P, t * P : (t + 1) * P],
+                rhs=codes[:, cols].bitcast(FP8X4),
+                rhs_scale=scales[:, cols],
+                start=start,
+                stop=False,
+            )
+
+        def wt_pass(n, t, a, operand, first, last):
+            codes, scales = operand
+            subs = WIDTHS[n] // SUB
+            for s in range(subs):
+                cols = slice(first + s * SUB, first + (s + 1) * SUB)
+                nc.tensor.matmul_mx(
+                    out=sum_of(n, t)[:, s * SUB : (s + 1) * SUB],
+                    lhsT=wt_d[:, (a * N + t * P) * 2 : (a * N + (t + 1) * P) * 2].bitcast(FP4X4),
+                    lhsT_scale=sc_d[:, a * N + t * P : a * N + (t + 1) * P],
+                    rhs=codes[:, cols].bitcast(FP8X4),
+                    rhs_scale=scales[:, cols],
+                    start=False,
+                    stop=last and s == subs - 1,
+                )
+
+        def open_sums(n):
+            h, first = divmod(STARTS[n], W)
+            cols = slice(first, first + WIDTHS[n])
+            per_bank = BANK // WIDTHS[n]
+            for u in range(PACK // per_bank):
+                banks[n, u] = psum.tile([P, per_bank, WIDTHS[n]], F32, name="acc", tag="bank")
+            for t in range(PACK):
+                wx_pass(n, t, cq[h], cols, t % per_bank == 0)
+            for t in range(PACK):
+                wx_pass(n, t, cr[h], cols, False)
+            for t in range(PACK):
+                wt_pass(n, t, 0, xq0[h], first, False)
+
+        out_rows = out_0.rearrange("(p t) j -> p t j", t=PACK)
+        out_words = out_1[0].rearrange("p j i -> p (j i)").bitcast(I32)
+        y_scales = held([P, J], U8, "y_scales")
+        picked1 = {}
+        xb1 = {}
+        yb = {}
+        picked1_at = [20, 36, 20, 36, 38]
+
+        def pick(n, i):
+            if i == 0:
+                picked1[n] = placed([P, PACK, WIDTHS[n]], F32, f"picked1_{n}", picked1_at[n])
+            gather(picked1[n][:, i, :], PACK + i, STARTS[n], STARTS[n] + WIDTHS[n])
+            if i == PACK - 1:
+                xb1[n] = held([P, PACK * WIDTHS[n]], BF16, f"xb1_{n}")
+                weave(xb1[n][:], picked1[n][:], n in X_ROUND_ON_VECTOR)
+
+        def close_sums(n):
+            per_bank = BANK // WIDTHS[n]
+            xq1 = quantize(xb1[n][:], f"xq1_{n}")
+            for t in range(PACK):
+                wt_pass(n, t, 1, xq1, 0, t % per_bank == per_bank - 1)
+            y = held([P, PACK, WIDTHS[n]], F32, f"y{n}")
+            for t in range(PACK):
+                nc.scalar.activation(out=y[:, t, :], in_=sum_of(n, t), func=ACT.Identity, bias=bias[:, t : t + 1])
+            nc.sync.dma_start(out_rows[:, :, STARTS[n] : STARTS[n] + WIDTHS[n]], y[:])
+            yb[n] = held([P, PACK * WIDTHS[n]], BF16, f"yb{n}")
+            weave(yb[n][:], y[:], n in Y_ROUND_ON_VECTOR)
+
+        def hand_on(n):
+            cols = slice(STARTS[n], STARTS[n] + WIDTHS[n])
+            y_codes = held([P, WIDTHS[n]], U32, f"y_codes{n}")
+            nc.vector.quantize_mx(out=y_codes[:].bitcast(FP8X4), scales=y_scales[:, cols], in_=yb[n][:])
+            nc.sync.dma_start(out_words[:, cols], y_codes[:].bitcast(I32))
+
+        for h in range(2):
+            leftover(2 + h)
+            quantize_first_pass(h)
+        for h in range(2):
+            second_tier(2 + h)
+        for n in range(2):
+            open_sums(n)
+        for i in range(PACK - 1):
+            pick(0, i)
+            if i < 2:
+                quantize_first_pass(2 + i)
+        for n in range(2, len(WIDTHS)):
+            open_sums(n)
+        pick(0, PACK - 1)
+        for step in range(1, len(WIDTHS) + 2):
+            if step < len(WIDTHS):
+                pick(step, 0)
+                pick(step, 1)
+            if step <= len(WIDTHS):
+                close_sums(step - 1)
+            if step < len(WIDTHS):
+                pick(step, 2)
+                pick(step, 3)
+            if step >= 2:
+                hand_on(step - 2)
+        for Q in range(4):
+            (nc.sync if Q % 2 == 0 else nc.scalar).dma_start(
+                out_2[0, 4 * Q : 4 * Q + 4, :].bitcast(I32), y_scales[32 * Q : 32 * Q + 4, :].bitcast(I32)
+            )

@@ -24,9 +24,7 @@ QUARTERS = J // W
 SUB = 128
 WIDTHS = [256, 256, 256, 128, 128]
 STARTS = [sum(WIDTHS[:n]) for n in range(len(WIDTHS))]
-X_ROUND_ON_VECTOR = ()
-Y_ROUND_ON_VECTOR = (1, 2, 3, 4)
-KB = 1024
+C_LOADS = [256, 256, 512]
 
 
 def tile_list_biasP_kernel(
@@ -35,14 +33,10 @@ def tile_list_biasP_kernel(
     nc = tc.nc
     with ExitStack() as ctx:
         keep = ctx.enter_context(tc.tile_pool(name="keep", bufs=1))
-        shared = ctx.enter_context(tc.tile_pool(name="shared", bufs=1))
         psum = ctx.enter_context(tc.psum_pool(name="psum", bufs=8))
 
         def held(shape, dtype, name):
             return keep.tile(shape, dtype, name=name, align_bytes=64)
-
-        def placed(shape, dtype, name, kib):
-            return shared.tile(shape, dtype, name=name, align_bytes=64, offset=kib * KB)
 
         def planar(t3):
             return t3.rearrange("p t (q i) -> p q t i", i=4)
@@ -68,17 +62,11 @@ def tile_list_biasP_kernel(
         wx_raw = held([P, N], I32, "wx_raw")
         sc_raw = held([P, 2, N], U8, "sc_raw")
         bias = held([P, PACK], F32, "bias")
-        wgt_first = placed([P, WIDTHS[0]], F32, "wgt_first", 36)
-        wgt_rest = held([P, J - WIDTHS[0]], F32, "wgt_rest")
-        x_at = {1: 24}
-        x_sb = [
-            placed([P, T], F32, f"x{k}", x_at[k]) if k in x_at else held([P, T], F32, f"x{k}")
-            for k in range(2 * PACK)
-        ]
-        c_at = [0, 4, 16, 20]
-        c_sb = [placed([P, PACK, W], F32, f"c{h}", c_at[h]) for h in range(QUARTERS)]
+        wgt_sb = held([P, J], F32, "wgt_sb")
+        x_sb = [held([P, T], F32, f"x{k}") for k in range(2 * PACK)]
+        c_sb = [held([P, PACK, w], F32, f"c{h}") for h, w in enumerate(C_LOADS)]
 
-        nc.vector.memset(sc_raw[:].bitcast(I32), 0)
+        nc.gpsimd.memset(sc_raw[:].bitcast(I32), 0)
         ones = held([P, P], F32, "ones")
         ramp = held([P, P], F32, "ramp")
         turned = held([P, P], F32, "turned")
@@ -104,43 +92,34 @@ def tile_list_biasP_kernel(
         wx_sc32 = wx_scales.bitcast(I32)
         sc32 = sc_raw[:].bitcast(I32)
 
+        def load_c(h):
+            j0 = sum(C_LOADS[:h])
+            return (c_sb[h][:], c_rows[:, :, j0 : j0 + C_LOADS[h]])
+
+        loads = [
+            load_c(0),
+            load_c(1),
+            (wt_raw[:].bitcast(I32), wt_words.bitcast(I32).rearrange("a p n -> p a n")),
+            (wx_raw[:], wx_words[0].rearrange("p n i -> p (n i)").bitcast(I32)),
+            load_c(2),
+            (offsets[:], offs),
+            (wgt_sb[:], wgt),
+        ]
         small = []
         for Q in range(4):
             small.append((sc32[32 * Q : 32 * Q + 4, :, :], wt_sc32[4 * Q : 4 * Q + 4, :, :]))
             small.append((sc32[32 * Q + 4 : 32 * Q + 8, 0, :], wx_sc32[0, 4 * Q : 4 * Q + 4, :]))
-
-        def load_x(k):
-            return (x_sb[k][:], x_planes[k // PACK, k % PACK])
-
-        def load_c(h):
-            return (c_sb[h][:], c_rows[:, :, h * W : (h + 1) * W])
-
-        loads = [
-            (wt_raw[:].bitcast(I32), wt_words.bitcast(I32).rearrange("a p n -> p a n")),
-            (wx_raw[:], wx_words[0].rearrange("p n i -> p (n i)").bitcast(I32)),
-            load_c(0),
-            load_c(1),
-            (offsets[:], offs),
-            (wgt_first[:], wgt[:, 0 : WIDTHS[0]]),
-            load_x(0),
-            (wgt_rest[:], wgt[:, WIDTHS[0] : J]),
-        ]
-        loads.extend(small[0:4] + [load_x(1)] + small[4:6] + [load_x(2)] + small[6:8] + [load_x(3)])
-        loads.extend([(bias[:], b.rearrange("(p t) -> p t", t=PACK)), load_c(2), load_c(3)])
-        loads.extend(load_x(k) for k in range(PACK, 2 * PACK))
+        small.append((bias[:], b.rearrange("(p t) -> p t", t=PACK)))
+        for k in range(2 * PACK):
+            loads.append((x_sb[k][:], x_planes[k // PACK, k % PACK]))
+            loads.extend(small[3 * k : 3 * k + 3])
         for dst, src in loads:
             nc.sync.dma_start(dst, src)
 
-        wt_d = held([P, 2 * 2 * N], U8, "wt_d")
-        nc.vector.tensor_copy(
-            out=wt_d[:].bitcast(U16).rearrange("p (a t m) -> p a t m", a=2, t=PACK),
-            in_=wt_raw[:].bitcast(U16).rearrange("p a (m t) -> p a t m", t=PACK),
-        )
-        wx_d = held([P, N], I32, "wx_d")
-        nc.vector.tensor_copy(
-            out=wx_d[:].rearrange("p (t q i) -> p q t i", t=PACK, i=4),
-            in_=wx_raw[:].rearrange("p (q i t) -> p q t i", t=PACK, i=4),
-        )
+        def c_cols(j0, j1):
+            h = max(u for u in range(len(C_LOADS)) if sum(C_LOADS[:u]) <= j0)
+            first = sum(C_LOADS[:h])
+            return c_sb[h][:, :, j0 - first : j1 - first]
 
         cb = {}
         cq = {}
@@ -148,8 +127,8 @@ def tile_list_biasP_kernel(
         rb = {}
 
         def round_c(h):
-            cb[h] = held([P, PACK * W], BF16, f"cb{h}") if h < 3 else placed([P, PACK * W], BF16, f"cb{h}", 40)
-            weave(cb[h][:], c_sb[h][:], False)
+            cb[h] = held([P, PACK * W], BF16, f"cb{h}")
+            weave(cb[h][:], c_cols(h * W, (h + 1) * W), h == 0)
 
         def first_tier(h):
             cq[h] = quantize(cb[h][:], f"cq{h}")
@@ -172,7 +151,7 @@ def tile_list_biasP_kernel(
                     )
                 nc.vector.tensor_tensor(
                     out=woven(rb[h][:, s * PACK * SUB : (s + 1) * PACK * SUB]),
-                    in0=planar(c_sb[h][:, :, cols]),
+                    in0=planar(c_cols(h * W + s * SUB, h * W + (s + 1) * SUB)),
                     in1=planar(back[:]),
                     op=ALU.subtract,
                 )
@@ -184,37 +163,35 @@ def tile_list_biasP_kernel(
             nc.vector.tensor_tensor(
                 out=dst,
                 in0=x_sb[k][:].indirect(offsets[:, j0 // 16 : j1 // 16]),
-                in1=wgt_first[:] if j0 == 0 else wgt_rest[:, j0 - WIDTHS[0] : j1 - WIDTHS[0]],
+                in1=wgt_sb[:, j0:j1],
                 op=ALU.mult,
             )
 
-        for h in range(2):
-            round_c(h)
-            first_tier(h)
-        for h in range(2):
-            leftover(h)
-        picked0 = placed([P, PACK, J], F32, "picked0", 0)
-        for i in range(PACK):
-            if i < 2:
-                second_tier(i)
-            gather(picked0[:, i, 0 : WIDTHS[0]], i, 0, WIDTHS[0])
-            gather(picked0[:, i, WIDTHS[0] : J], i, WIDTHS[0], J)
-            if i == 2:
-                sc_d = placed([P, 2 * N], U8, "sc_d", 24)
-                nc.vector.tensor_copy(
-                    out=sc_d[:].rearrange("p (a t m) -> p a t m", a=2, t=PACK),
-                    in_=sc_raw[:].rearrange("p a (m t) -> p a t m", t=PACK),
-                )
-        for h in range(2, QUARTERS):
-            round_c(h)
-            first_tier(h)
-        xb0 = placed([P, PACK * J], BF16, "xb0", 40)
         for h in range(QUARTERS):
-            weave(xb0[:, h * PACK * W : (h + 1) * PACK * W], picked0[:, :, h * W : (h + 1) * W], False)
-        xq0 = {}
+            round_c(h)
+        for h in range(QUARTERS + 2):
+            if h < QUARTERS:
+                first_tier(h)
+            if 1 <= h <= QUARTERS:
+                leftover(h - 1)
+            if h >= 2:
+                second_tier(h - 2)
 
-        def quantize_first_pass(h):
-            xq0[h] = quantize(xb0[:, h * PACK * W : (h + 1) * PACK * W], f"xq0_{h}")
+        wt_d = held([P, 2 * 2 * N], U8, "wt_d")
+        nc.vector.tensor_copy(
+            out=wt_d[:].bitcast(U16).rearrange("p (a t m) -> p a t m", a=2, t=PACK),
+            in_=wt_raw[:].bitcast(U16).rearrange("p a (m t) -> p a t m", t=PACK),
+        )
+        wx_d = held([P, N], I32, "wx_d")
+        nc.vector.tensor_copy(
+            out=wx_d[:].rearrange("p (t q i) -> p q t i", t=PACK, i=4),
+            in_=wx_raw[:].rearrange("p (q i t) -> p q t i", t=PACK, i=4),
+        )
+        sc_d = held([P, 2 * N], U8, "sc_d")
+        nc.vector.tensor_copy(
+            out=sc_d[:].rearrange("p (a t m) -> p a t m", a=2, t=PACK),
+            in_=sc_raw[:].rearrange("p a (m t) -> p a t m", t=PACK),
+        )
 
         banks = {}
 
@@ -249,7 +226,7 @@ def tile_list_biasP_kernel(
                     stop=last and s == subs - 1,
                 )
 
-        def open_sums(n):
+        for n in range(len(WIDTHS)):
             h, first = divmod(STARTS[n], W)
             cols = slice(first, first + WIDTHS[n])
             per_bank = BANK // WIDTHS[n]
@@ -259,36 +236,58 @@ def tile_list_biasP_kernel(
                 wx_pass(n, t, cq[h], cols, t % per_bank == 0)
             for t in range(PACK):
                 wx_pass(n, t, cr[h], cols, False)
+
+        picked0 = held([P, PACK, J], F32, "picked0")
+        picked1 = held([P, PACK, J], F32, "picked1")
+        for k in range(PACK):
+            gather(picked0[:, k, :], k, 0, J)
+        xb0 = [held([P, PACK * W], BF16, f"xb0_{h}") for h in range(QUARTERS)]
+        for h in range(QUARTERS):
+            weave(xb0[h][:], picked0[:, :, h * W : (h + 1) * W], False)
+        xb1 = [held([P, w, PACK], BF16, f"xb1_{n}") for n, w in enumerate(WIDTHS)]
+
+        def weave_pair(n, t0):
+            nc.scalar.activation(
+                out=xb1[n][:, :, t0 : t0 + 2],
+                in_=picked1[:, t0 : t0 + 2, STARTS[n] : STARTS[n] + WIDTHS[n]].rearrange("p t j -> p j t"),
+                func=ACT.Identity,
+            )
+
+        xq0 = {}
+        for k in range(PACK - 1):
+            gather(picked1[:, k, :], PACK + k, 0, J)
+            if k < 2:
+                for h in (2 * k, 2 * k + 1):
+                    xq0[h] = quantize(xb0[h][:], f"xq0_{h}")
+        for n in range(len(WIDTHS)):
+            h, first = divmod(STARTS[n], W)
             for t in range(PACK):
                 wt_pass(n, t, 0, xq0[h], first, False)
+            weave_pair(n, 0)
 
         out_rows = out_0.rearrange("(p t) j -> p t j", t=PACK)
         out_words = out_1[0].rearrange("p j i -> p (j i)").bitcast(I32)
         y_scales = held([P, J], U8, "y_scales")
-        picked1 = {}
-        xb1 = {}
+        y = {}
         yb = {}
-        picked1_at = [20, 36, 20, 36, 38]
 
-        def pick(n, i):
-            if i == 0:
-                picked1[n] = placed([P, PACK, WIDTHS[n]], F32, f"picked1_{n}", picked1_at[n])
-            gather(picked1[n][:, i, :], PACK + i, STARTS[n], STARTS[n] + WIDTHS[n])
-            if i == PACK - 1:
-                xb1[n] = held([P, PACK * WIDTHS[n]], BF16, f"xb1_{n}")
-                weave(xb1[n][:], picked1[n][:], n in X_ROUND_ON_VECTOR)
+        def pick(n):
+            gather(picked1[:, PACK - 1, STARTS[n] : STARTS[n] + WIDTHS[n]], 2 * PACK - 1, STARTS[n], STARTS[n] + WIDTHS[n])
+            weave_pair(n, 2)
 
         def close_sums(n):
             per_bank = BANK // WIDTHS[n]
-            xq1 = quantize(xb1[n][:], f"xq1_{n}")
+            xq1 = quantize(xb1[n][:].rearrange("p j t -> p (j t)"), f"xq1_{n}")
             for t in range(PACK):
                 wt_pass(n, t, 1, xq1, 0, t % per_bank == per_bank - 1)
-            y = held([P, PACK, WIDTHS[n]], F32, f"y{n}")
+            y[n] = held([P, PACK, WIDTHS[n]], F32, f"y{n}")
             for t in range(PACK):
-                nc.scalar.activation(out=y[:, t, :], in_=sum_of(n, t), func=ACT.Identity, bias=bias[:, t : t + 1])
-            nc.sync.dma_start(out_rows[:, :, STARTS[n] : STARTS[n] + WIDTHS[n]], y[:])
+                nc.scalar.activation(out=y[n][:, t, :], in_=sum_of(n, t), func=ACT.Identity, bias=bias[:, t : t + 1])
+            nc.sync.dma_start(out_rows[:, :, STARTS[n] : STARTS[n] + WIDTHS[n]], y[n][:])
+
+        def round_y(n):
             yb[n] = held([P, PACK * WIDTHS[n]], BF16, f"yb{n}")
-            weave(yb[n][:], y[:], n in Y_ROUND_ON_VECTOR)
+            weave(yb[n][:], y[n][:], True)
 
         def hand_on(n):
             cols = slice(STARTS[n], STARTS[n] + WIDTHS[n])
@@ -296,31 +295,15 @@ def tile_list_biasP_kernel(
             nc.vector.quantize_mx(out=y_codes[:].bitcast(FP8X4), scales=y_scales[:, cols], in_=yb[n][:])
             nc.sync.dma_start(out_words[:, cols], y_codes[:].bitcast(I32))
 
-        for h in range(2):
-            leftover(2 + h)
-            quantize_first_pass(h)
-        for h in range(2):
-            second_tier(2 + h)
-        for n in range(2):
-            open_sums(n)
-        for i in range(PACK - 1):
-            pick(0, i)
-            if i < 2:
-                quantize_first_pass(2 + i)
-        for n in range(2, len(WIDTHS)):
-            open_sums(n)
-        pick(0, PACK - 1)
-        for step in range(1, len(WIDTHS) + 2):
+        for step in range(len(WIDTHS) + 3):
             if step < len(WIDTHS):
-                pick(step, 0)
-                pick(step, 1)
-            if step <= len(WIDTHS):
+                pick(step)
+            if 1 <= step <= len(WIDTHS):
                 close_sums(step - 1)
-            if step < len(WIDTHS):
-                pick(step, 2)
-                pick(step, 3)
-            if step >= 2:
-                hand_on(step - 2)
+            if step >= 3:
+                hand_on(step - 3)
+            if 2 <= step <= len(WIDTHS) + 1:
+                round_y(step - 2)
         for Q in range(4):
             (nc.sync if Q % 2 == 0 else nc.scalar).dma_start(
                 out_2[0, 4 * Q : 4 * Q + 4, :].bitcast(I32), y_scales[32 * Q : 32 * Q + 4, :].bitcast(I32)

@@ -24,7 +24,10 @@ QUARTERS = J // W
 SUB = 128
 WIDTHS = [256, 256, 256, 128, 128]
 STARTS = [sum(WIDTHS[:n]) for n in range(len(WIDTHS))]
-C_LOADS = [256, 256, 512]
+C_LOADS = [256, 256, 256, 256]
+Y_ROUND_ON_SCALAR = ()
+X_ROUND_ON_VECTOR = (3, 4)
+IN_PSUM = (2, 3)
 
 
 def tile_list_biasP_kernel(
@@ -33,10 +36,21 @@ def tile_list_biasP_kernel(
     nc = tc.nc
     with ExitStack() as ctx:
         keep = ctx.enter_context(tc.tile_pool(name="keep", bufs=1))
+        shared = ctx.enter_context(tc.tile_pool(name="shared", bufs=1))
         psum = ctx.enter_context(tc.psum_pool(name="psum", bufs=8))
 
         def held(shape, dtype, name):
             return keep.tile(shape, dtype, name=name, align_bytes=64)
+
+        def placed(shape, dtype, name, kib):
+            return shared.tile(shape, dtype, name=name, align_bytes=64, offset=int(kib * 1024))
+
+        def operand(name):
+            return held([P, J], U32, name + "_codes"), held([P, J], U8, name + "_scales")
+
+        def quantize_into(dst, j0, src):
+            cols = slice(j0, j0 + src.shape[1] // PACK)
+            nc.vector.quantize_mx(out=dst[0][:, cols].bitcast(FP8X4), scales=dst[1][:, cols], in_=src)
 
         def planar(t3):
             return t3.rearrange("p t (q i) -> p q t i", i=4)
@@ -63,27 +77,33 @@ def tile_list_biasP_kernel(
         sc_raw = held([P, 2, N], U8, "sc_raw")
         bias = held([P, PACK], F32, "bias")
         wgt_sb = held([P, J], F32, "wgt_sb")
-        x_sb = [held([P, T], F32, f"x{k}") for k in range(2 * PACK)]
+        x_sb = [placed([P, T], F32, f"x{k}", 0) if k == PACK else held([P, T], F32, f"x{k}") for k in range(2 * PACK)]
         c_sb = [held([P, PACK, w], F32, f"c{h}") for h, w in enumerate(C_LOADS)]
 
-        nc.gpsimd.memset(sc_raw[:].bitcast(I32), 0)
+        eye = held([P, PACK * (L + 1)], BF16, "eye")
         ones = held([P, P], F32, "ones")
         ramp = held([P, P], F32, "ramp")
-        turned = held([P, P], F32, "turned")
-        eye = held([P, PACK * (L + 1)], BF16, "eye")
+        base = held([P, 1], F32, "base")
+        turned = held([P, 32], F32, "turned")
+        nc.gpsimd.memset(eye[:].bitcast(I32), 0)
         nc.vector.memset(ones[:], 1.0)
-        nc.vector.memset(eye[:].bitcast(I32), 0)
-        nc.vector.tensor_tensor_scan(out=ramp[:], data0=ones[:], data1=ones[:], initial=0.0, op0=ALU.mult, op1=ALU.add)
-        nc.vector.transpose(out=turned[:], in_=ramp[:])
-        eye_rows = eye[:].rearrange("p (t x) -> p t x", t=PACK)
         for Q in range(4):
-            rows = slice(32 * Q, 32 * Q + 32)
-            nc.vector.tensor_tensor(
-                out=eye_rows[rows, :, P * Q : P * (Q + 1) : PACK],
-                in0=ramp[rows, :].rearrange("p (t m) -> p t m", t=PACK),
-                in1=turned[rows, :].rearrange("p (t m) -> p t m", t=PACK),
-                op=ALU.is_equal,
-            )
+            nc.vector.memset(base[32 * Q : 32 * Q + 32, :], float(32 * Q))
+        nc.vector.tensor_tensor_scan(out=ramp[:], data0=ones[:], data1=ones[:], initial=0.0, op0=ALU.mult, op1=ALU.add)
+        nc.vector.transpose(out=turned[:], in_=ramp[:, 0:32])
+        nc.vector.tensor_scalar(
+            out=eye[:].rearrange("p (t x) -> p t x", t=PACK)[:, :, 0:L:PACK],
+            in0=ramp[:].unsqueeze(1).to_broadcast([P, PACK, P]),
+            scalar1=base[:],
+            scalar2=turned[:, 0:1],
+            op0=ALU.subtract,
+            op1=ALU.is_equal,
+        )
+        ident = held([P, P], F32, "ident")
+        nc.vector.tensor_scalar(
+            out=ident[:], in0=ramp[:], scalar1=base[:], scalar2=turned[:, 0:1], op0=ALU.subtract, op1=ALU.is_equal
+        )
+        nc.gpsimd.memset(sc_raw[:].bitcast(I32), 0)
         eye_codes, eye_scales = quantize(eye[:, 0 : PACK * L], "eye")
 
         x_planes = xT.rearrange("(a p i) t -> a i p t", a=2, i=PACK)
@@ -98,10 +118,11 @@ def tile_list_biasP_kernel(
 
         loads = [
             load_c(0),
-            load_c(1),
             (wt_raw[:].bitcast(I32), wt_words.bitcast(I32).rearrange("a p n -> p a n")),
+            load_c(1),
             (wx_raw[:], wx_words[0].rearrange("p n i -> p (n i)").bitcast(I32)),
             load_c(2),
+            load_c(3),
             (offsets[:], offs),
             (wgt_sb[:], wgt),
         ]
@@ -122,22 +143,23 @@ def tile_list_biasP_kernel(
             return c_sb[h][:, :, j0 - first : j1 - first]
 
         cb = {}
-        cq = {}
+        cq = operand("cq")
         cr = {}
-        rb = {}
+        rb = [held([P, 2 * PACK * W], BF16, f"rb{u}") for u in range(2)]
 
         def round_c(h):
             cb[h] = held([P, PACK * W], BF16, f"cb{h}")
             weave(cb[h][:], c_cols(h * W, (h + 1) * W), h == 0)
 
         def first_tier(h):
-            cq[h] = quantize(cb[h][:], f"cq{h}")
+            quantize_into(cq, h * W, cb[h][:])
 
         def leftover(h):
-            codes, scales = cq[h]
-            rb[h] = held([P, PACK * W], BF16, f"rb{h}")
+            codes, scales = cq
+            backs = []
             for s in range(W // SUB):
-                cols = slice(s * SUB, (s + 1) * SUB)
+                cols = slice(h * W + s * SUB, h * W + (s + 1) * SUB)
+                at = (h % 2 * W + s * SUB) * PACK
                 back = psum.tile([P, PACK, SUB], F32, name="back", tag="bank")
                 for t in range(PACK):
                     nc.tensor.matmul_mx(
@@ -149,15 +171,59 @@ def tile_list_biasP_kernel(
                         start=True,
                         stop=True,
                     )
-                nc.vector.tensor_tensor(
-                    out=woven(rb[h][:, s * PACK * SUB : (s + 1) * PACK * SUB]),
-                    in0=planar(c_cols(h * W + s * SUB, h * W + (s + 1) * SUB)),
-                    in1=planar(back[:]),
-                    op=ALU.subtract,
+                if h in IN_PSUM:
+                    backs.append(back)
+                else:
+                    nc.vector.tensor_tensor(
+                        out=woven(rb[h // 2][:, at : at + PACK * SUB]),
+                        in0=planar(c_cols(h * W + s * SUB, h * W + (s + 1) * SUB)),
+                        in1=planar(back[:]),
+                        op=ALU.subtract,
+                    )
+            if h in IN_PSUM:
+                leftover_in_psum(h, backs)
+
+        def leftover_in_psum(h, backs):
+            minus = []
+            for s, back in enumerate(backs):
+                minus.append(held([P, PACK, SUB], F32, f"minus{h}_{s}"))
+                nc.scalar.activation(out=minus[s][:], in_=back[:], func=ACT.Identity, scale=-1.0)
+            pairs = []
+            for s in range(W // SUB):
+                rest = psum.tile([P, PACK, P], F32, name="rest", tag="bank")
+                src = c_cols(h * W + s * SUB, h * W + (s + 1) * SUB)
+                for t in range(PACK):
+                    nc.tensor.matmul(
+                        rest[:, t, :], lhsT=src[:, t, :], rhs=ident[:], is_transpose=True, start=t == 0, stop=False
+                    )
+                for t in range(PACK):
+                    nc.tensor.matmul(
+                        rest[:, t, :],
+                        lhsT=minus[s][:, t, :],
+                        rhs=ident[:],
+                        is_transpose=True,
+                        start=False,
+                        stop=t == PACK - 1,
+                    )
+                pairs.append(held([P, 2, P, 2], BF16, f"pairs{h}_{s}"))
+                nc.scalar.activation(
+                    out=pairs[s][:], in_=rest[:].rearrange("j (u e) p -> j u p e", e=2), func=ACT.Identity
                 )
+            words = psum.tile([P, W // SUB, 2, SUB], F32, name="words", tag="bank")
+            for s in range(W // SUB):
+                as_words = pairs[s][:].rearrange("j u p e -> j (u p e)").bitcast(F32)
+                for u in range(2):
+                    nc.tensor.transpose(words[:, s, u, :], as_words[:, u * P : (u + 1) * P], ident[:])
+            at = h % 2 * W * PACK
+            nc.scalar.copy(
+                out=rb[h // 2][:, at : at + PACK * W].bitcast(F32).rearrange("p (s j u) -> p s j u", s=W // SUB, u=2),
+                in_=words[:].rearrange("p s u j -> p s j u"),
+            )
 
         def second_tier(h):
-            cr[h] = quantize(rb[h][:], f"cr{h}")
+            codes = placed([P, 2 * W], U32, "cr_late", 0) if h else held([P, 2 * W], U32, "cr_early")
+            cr[h] = (codes, held([P, 2 * W], U8, f"cr_scales{h}"))
+            quantize_into(cr[h], 0, rb[h][:])
 
         def gather(dst, k, j0, j1):
             nc.vector.tensor_tensor(
@@ -174,8 +240,8 @@ def tile_list_biasP_kernel(
                 first_tier(h)
             if 1 <= h <= QUARTERS:
                 leftover(h - 1)
-            if h >= 2:
-                second_tier(h - 2)
+            if h == 3:
+                second_tier(0)
 
         wt_d = held([P, 2 * 2 * N], U8, "wt_d")
         nc.vector.tensor_copy(
@@ -211,11 +277,11 @@ def tile_list_biasP_kernel(
                 stop=False,
             )
 
-        def wt_pass(n, t, a, operand, first, last):
-            codes, scales = operand
+        def wt_pass(n, t, a, operand, last):
             subs = WIDTHS[n] // SUB
             for s in range(subs):
-                cols = slice(first + s * SUB, first + (s + 1) * SUB)
+                codes, scales, first = operand[STARTS[n] + s * SUB]
+                cols = slice(first, first + SUB)
                 nc.tensor.matmul_mx(
                     out=sum_of(n, t)[:, s * SUB : (s + 1) * SUB],
                     lhsT=wt_d[:, (a * N + t * P) * 2 : (a * N + (t + 1) * P) * 2].bitcast(FP4X4),
@@ -226,84 +292,127 @@ def tile_list_biasP_kernel(
                     stop=last and s == subs - 1,
                 )
 
-        for n in range(len(WIDTHS)):
-            h, first = divmod(STARTS[n], W)
-            cols = slice(first, first + WIDTHS[n])
+        def open_sums(n):
+            cols = slice(STARTS[n], STARTS[n] + WIDTHS[n])
             per_bank = BANK // WIDTHS[n]
             for u in range(PACK // per_bank):
                 banks[n, u] = psum.tile([P, per_bank, WIDTHS[n]], F32, name="acc", tag="bank")
             for t in range(PACK):
-                wx_pass(n, t, cq[h], cols, t % per_bank == 0)
+                wx_pass(n, t, cq, cols, t % per_bank == 0)
+
+        def add_second_tier(n):
+            half, first = divmod(STARTS[n], 2 * W)
             for t in range(PACK):
-                wx_pass(n, t, cr[h], cols, False)
+                wx_pass(n, t, cr[half], slice(first, first + WIDTHS[n]), False)
+
+        for n in range(len(WIDTHS)):
+            open_sums(n)
+            if STARTS[n] < 2 * W:
+                add_second_tier(n)
 
         picked0 = held([P, PACK, J], F32, "picked0")
-        picked1 = held([P, PACK, J], F32, "picked1")
         for k in range(PACK):
-            gather(picked0[:, k, :], k, 0, J)
-        xb0 = [held([P, PACK * W], BF16, f"xb0_{h}") for h in range(QUARTERS)]
-        for h in range(QUARTERS):
-            weave(xb0[h][:], picked0[:, :, h * W : (h + 1) * W], False)
-        xb1 = [held([P, w, PACK], BF16, f"xb1_{n}") for n, w in enumerate(WIDTHS)]
-
-        def weave_pair(n, t0):
-            nc.scalar.activation(
-                out=xb1[n][:, :, t0 : t0 + 2],
-                in_=picked1[:, t0 : t0 + 2, STARTS[n] : STARTS[n] + WIDTHS[n]].rearrange("p t j -> p j t"),
-                func=ACT.Identity,
-            )
+            cuts = [0] + ([J // 2] if k == PACK - 1 else []) + [J]
+            for j0, j1 in zip(cuts, cuts[1:]):
+                gather(picked0[:, k, j0:j1], k, j0, j1)
+        xb0 = [held([P, 2 * PACK * W], BF16, f"xb0_{u}") for u in range(2)]
+        for u in range(2):
+            weave(xb0[u][:], picked0[:, :, u * 2 * W : (u + 1) * 2 * W], False)
 
         xq0 = {}
-        for k in range(PACK - 1):
-            gather(picked1[:, k, :], PACK + k, 0, J)
-            if k < 2:
-                for h in (2 * k, 2 * k + 1):
-                    xq0[h] = quantize(xb0[h][:], f"xq0_{h}")
-        for n in range(len(WIDTHS)):
-            h, first = divmod(STARTS[n], W)
-            for t in range(PACK):
-                wt_pass(n, t, 0, xq0[h], first, False)
-            weave_pair(n, 0)
+
+        def first_pass(u):
+            codes, scales = quantize(xb0[u][:], f"xq0_{u}")
+            for j0 in range(u * 2 * W, (u + 1) * 2 * W, SUB):
+                xq0[j0] = (codes, scales, j0 - u * 2 * W)
+            for n in range(len(WIDTHS)):
+                if STARTS[n] // (2 * W) == u:
+                    for t in range(PACK):
+                        wt_pass(n, t, 0, xq0, False)
 
         out_rows = out_0.rearrange("(p t) j -> p t j", t=PACK)
         out_words = out_1[0].rearrange("p j i -> p (j i)").bitcast(I32)
         y_scales = held([P, J], U8, "y_scales")
-        y = {}
-        yb = {}
+        stage = held([P, PACK * J + W], F32, "stage")
+        picked1 = stage[:, 0 : PACK * J].rearrange("p (t j) -> p t j", t=PACK)
+        xb1 = {
+            0: stage[:, 2 * J + 2 * W : 3 * J].bitcast(BF16),
+            1: stage[:, 3 * J + 3 * W : PACK * J + W].bitcast(BF16),
+        }
+        for n in range(2, len(WIDTHS)):
+            xb1[n] = held([P, PACK * WIDTHS[n]], BF16, f"xb1_{n}")[:]
+        y = [held([P, PACK, W], F32, f"y{h}") for h in range(QUARTERS)]
+        yb = [held([P, PACK * W], BF16, f"yb{h}") for h in range(QUARTERS)]
 
-        def pick(n):
-            gather(picked1[:, PACK - 1, STARTS[n] : STARTS[n] + WIDTHS[n]], 2 * PACK - 1, STARTS[n], STARTS[n] + WIDTHS[n])
-            weave_pair(n, 2)
+        def pick(i, j0, j1):
+            gather(picked1[:, i, j0:j1], PACK + i, j0, j1)
+
+        def pick_last(n):
+            pick(PACK - 1, STARTS[n], STARTS[n] + WIDTHS[n])
+
+        def round_x(n):
+            weave(xb1[n], picked1[:, :, STARTS[n] : STARTS[n] + WIDTHS[n]], n in X_ROUND_ON_VECTOR)
 
         def close_sums(n):
             per_bank = BANK // WIDTHS[n]
-            xq1 = quantize(xb1[n][:].rearrange("p j t -> p (j t)"), f"xq1_{n}")
+            codes, scales = quantize(xb1[n], f"xq1_{n}")
+            xq1 = {STARTS[n] + j: (codes, scales, j) for j in range(0, WIDTHS[n], SUB)}
             for t in range(PACK):
-                wt_pass(n, t, 1, xq1, 0, t % per_bank == per_bank - 1)
-            y[n] = held([P, PACK, WIDTHS[n]], F32, f"y{n}")
+                wt_pass(n, t, 1, xq1, t % per_bank == per_bank - 1)
+
+        def add_bias(n):
+            h, first = divmod(STARTS[n], W)
             for t in range(PACK):
-                nc.scalar.activation(out=y[n][:, t, :], in_=sum_of(n, t), func=ACT.Identity, bias=bias[:, t : t + 1])
-            nc.sync.dma_start(out_rows[:, :, STARTS[n] : STARTS[n] + WIDTHS[n]], y[n][:])
+                dst = y[h][:, t, first : first + WIDTHS[n]]
+                nc.scalar.activation(out=dst, in_=sum_of(n, t), func=ACT.Identity, bias=bias[:, t : t + 1])
+                if n == 0 and t % 2 == 1:
+                    nc.sync.dma_start(out_rows[:, t - 1 : t + 1, 0:W], y[0][:, t - 1 : t + 1, :])
+            if n > 0 and first + WIDTHS[n] == W:
+                nc.sync.dma_start(out_rows[:, :, h * W : (h + 1) * W], y[h][:])
 
         def round_y(n):
-            yb[n] = held([P, PACK * WIDTHS[n]], BF16, f"yb{n}")
-            weave(yb[n][:], y[n][:], True)
+            h, first = divmod(STARTS[n], W)
+            dst = yb[h][:, PACK * first : PACK * (first + WIDTHS[n])]
+            weave(dst, y[h][:, :, first : first + WIDTHS[n]], n not in Y_ROUND_ON_SCALAR)
 
         def hand_on(n):
-            cols = slice(STARTS[n], STARTS[n] + WIDTHS[n])
-            y_codes = held([P, WIDTHS[n]], U32, f"y_codes{n}")
+            cols = slice(n * W, (n + 1) * W)
+            y_codes = held([P, W], U32, f"y_codes{n}")
             nc.vector.quantize_mx(out=y_codes[:].bitcast(FP8X4), scales=y_scales[:, cols], in_=yb[n][:])
             nc.sync.dma_start(out_words[:, cols], y_codes[:].bitcast(I32))
 
-        for step in range(len(WIDTHS) + 3):
+        pick(0, 0, J)
+        first_pass(0)
+        second_tier(1)
+        for n in range(2, len(WIDTHS)):
+            add_second_tier(n)
+        pick(1, 0, J)
+        first_pass(1)
+        pick(2, 0, 2 * W)
+        for n in range(3):
+            pick_last(n)
+        round_x(0)
+        round_x(1)
+        close_sums(0)
+        add_bias(0)
+        pick(2, 2 * W, 3 * W)
+        round_x(2)
+        pick(2, 3 * W, J)
+        close_sums(1)
+        pick_last(3)
+        pick_last(4)
+        round_x(3)
+        close_sums(2)
+        round_x(4)
+        close_sums(3)
+        close_sums(4)
+        for n in range(1, len(WIDTHS)):
+            add_bias(n)
+        for step in range(len(WIDTHS) + 1):
             if step < len(WIDTHS):
-                pick(step)
-            if 1 <= step <= len(WIDTHS):
-                close_sums(step - 1)
-            if step >= 3:
-                hand_on(step - 3)
-            if 2 <= step <= len(WIDTHS) + 1:
-                round_y(step - 2)
+                round_y(step)
+            if step in (1, 2, 3, 5):
+                hand_on(min(step - 1, QUARTERS - 1))
         for Q in range(4):
             (nc.sync if Q % 2 == 0 else nc.scalar).dma_start(
                 out_2[0, 4 * Q : 4 * Q + 4, :].bitcast(I32), y_scales[32 * Q : 32 * Q + 4, :].bitcast(I32)

@@ -24,9 +24,9 @@ QUARTERS = J // W
 SUB = 128
 WIDTHS = [256, 256, 256, 128, 128]
 STARTS = [sum(WIDTHS[:n]) for n in range(len(WIDTHS))]
-C_LOADS = [256, 256, 256, 256]
-Y_ROUND_ON_SCALAR = ()
-X_ROUND_ON_VECTOR = (3, 4)
+C_LOADS = [256, 256, 512]
+Y_ROUND_ON_SCALAR = (0,)
+X_ROUND_ON_VECTOR = (2, 3, 4)
 IN_PSUM = (2, 3)
 
 
@@ -120,9 +120,6 @@ def tile_list_biasP_kernel(
             load_c(0),
             (wt_raw[:].bitcast(I32), wt_words.bitcast(I32).rearrange("a p n -> p a n")),
             load_c(1),
-            (wx_raw[:], wx_words[0].rearrange("p n i -> p (n i)").bitcast(I32)),
-            load_c(2),
-            load_c(3),
             (offsets[:], offs),
             (wgt_sb[:], wgt),
         ]
@@ -133,6 +130,9 @@ def tile_list_biasP_kernel(
         small.append((bias[:], b.rearrange("(p t) -> p t", t=PACK)))
         for k in range(2 * PACK):
             loads.append((x_sb[k][:], x_planes[k // PACK, k % PACK]))
+            if k == 0:
+                loads.append((wx_raw[:], wx_words[0].rearrange("p n i -> p (n i)").bitcast(I32)))
+                loads.append(load_c(2))
             loads.extend(small[3 * k : 3 * k + 3])
         for dst, src in loads:
             nc.sync.dma_start(dst, src)
@@ -245,8 +245,8 @@ def tile_list_biasP_kernel(
 
         wt_d = held([P, 2 * 2 * N], U8, "wt_d")
         nc.vector.tensor_copy(
-            out=wt_d[:].bitcast(U16).rearrange("p (a t m) -> p a t m", a=2, t=PACK),
-            in_=wt_raw[:].bitcast(U16).rearrange("p a (m t) -> p a t m", t=PACK),
+            out=wt_d[:].bitcast(U16).rearrange("p (a t q i) -> p a q t i", a=2, t=PACK, i=8),
+            in_=wt_raw[:].bitcast(U16).rearrange("p a (q i t) -> p a q t i", t=PACK, i=8),
         )
         wx_d = held([P, N], I32, "wx_d")
         nc.vector.tensor_copy(
@@ -255,8 +255,8 @@ def tile_list_biasP_kernel(
         )
         sc_d = held([P, 2 * N], U8, "sc_d")
         nc.vector.tensor_copy(
-            out=sc_d[:].rearrange("p (a t m) -> p a t m", a=2, t=PACK),
-            in_=sc_raw[:].rearrange("p a (m t) -> p a t m", t=PACK),
+            out=sc_d[:].rearrange("p (a t q i) -> p a q t i", a=2, t=PACK, i=16),
+            in_=sc_raw[:].rearrange("p a (q i t) -> p a q t i", t=PACK, i=16),
         )
 
         banks = {}
@@ -333,11 +333,11 @@ def tile_list_biasP_kernel(
         out_rows = out_0.rearrange("(p t) j -> p t j", t=PACK)
         out_words = out_1[0].rearrange("p j i -> p (j i)").bitcast(I32)
         y_scales = held([P, J], U8, "y_scales")
-        stage = held([P, PACK * J + W], F32, "stage")
-        picked1 = stage[:, 0 : PACK * J].rearrange("p (t j) -> p t j", t=PACK)
+        stage = held([P, PACK * J], F32, "stage")
+        picked1 = stage[:].rearrange("p (t j) -> p t j", t=PACK)
         xb1 = {
             0: stage[:, 2 * J + 2 * W : 3 * J].bitcast(BF16),
-            1: stage[:, 3 * J + 3 * W : PACK * J + W].bitcast(BF16),
+            1: stage[:, J + 2 * W : 2 * J].bitcast(BF16),
         }
         for n in range(2, len(WIDTHS)):
             xb1[n] = held([P, PACK * WIDTHS[n]], BF16, f"xb1_{n}")[:]
@@ -346,9 +346,6 @@ def tile_list_biasP_kernel(
 
         def pick(i, j0, j1):
             gather(picked1[:, i, j0:j1], PACK + i, j0, j1)
-
-        def pick_last(n):
-            pick(PACK - 1, STARTS[n], STARTS[n] + WIDTHS[n])
 
         def round_x(n):
             weave(xb1[n], picked1[:, :, STARTS[n] : STARTS[n] + WIDTHS[n]], n in X_ROUND_ON_VECTOR)
@@ -386,27 +383,28 @@ def tile_list_biasP_kernel(
         second_tier(1)
         for n in range(2, len(WIDTHS)):
             add_second_tier(n)
-        pick(1, 0, J)
+        pick(1, 0, 2 * W)
         first_pass(1)
         pick(2, 0, 2 * W)
-        for n in range(3):
-            pick_last(n)
+        pick(3, 0, W)
+        pick(3, W, 2 * W)
+        pick(3, 2 * W, J)
         round_x(0)
         round_x(1)
         close_sums(0)
         add_bias(0)
-        pick(2, 2 * W, 3 * W)
-        round_x(2)
-        pick(2, 3 * W, J)
+        pick(2, 2 * W, J)
         close_sums(1)
-        pick_last(3)
-        pick_last(4)
-        round_x(3)
+        add_bias(1)
+        pick(1, 2 * W, 3 * W)
+        round_x(2)
+        pick(1, 3 * W, J)
         close_sums(2)
+        round_x(3)
         round_x(4)
         close_sums(3)
         close_sums(4)
-        for n in range(1, len(WIDTHS)):
+        for n in range(2, len(WIDTHS)):
             add_bias(n)
         for step in range(len(WIDTHS) + 1):
             if step < len(WIDTHS):

@@ -77,7 +77,7 @@ def tile_list_biasP_kernel(
         sc_raw = held([P, 2, N], U8, "sc_raw")
         bias = held([P, PACK], F32, "bias")
         wgt_sb = held([P, J], F32, "wgt_sb")
-        x_sb = [placed([P, T], F32, f"x{k}", 0) if k == PACK else held([P, T], F32, f"x{k}") for k in range(2 * PACK)]
+        x_sb = [placed([P, T], F32, f"x{k}", 0) if k == PACK + 2 else held([P, T], F32, f"x{k}") for k in range(2 * PACK)]
         c_sb = [held([P, PACK, w], F32, f"c{h}") for h, w in enumerate(C_LOADS)]
 
         eye = held([P, PACK * (L + 1)], BF16, "eye")
@@ -116,24 +116,20 @@ def tile_list_biasP_kernel(
             j0 = sum(C_LOADS[:h])
             return (c_sb[h][:], c_rows[:, :, j0 : j0 + C_LOADS[h]])
 
-        loads = [
-            load_c(0),
-            (wt_raw[:].bitcast(I32), wt_words.bitcast(I32).rearrange("a p n -> p a n")),
-            load_c(1),
-            (offsets[:], offs),
-            (wgt_sb[:], wgt),
-        ]
         small = []
         for Q in range(4):
             small.append((sc32[32 * Q : 32 * Q + 4, :, :], wt_sc32[4 * Q : 4 * Q + 4, :, :]))
             small.append((sc32[32 * Q + 4 : 32 * Q + 8, 0, :], wx_sc32[0, 4 * Q : 4 * Q + 4, :]))
-        small.append((bias[:], b.rearrange("(p t) -> p t", t=PACK)))
-        for k in range(2 * PACK):
-            loads.append((x_sb[k][:], x_planes[k // PACK, k % PACK]))
-            if k == 0:
-                loads.append((wx_raw[:], wx_words[0].rearrange("p n i -> p (n i)").bitcast(I32)))
-                loads.append(load_c(2))
-            loads.extend(small[3 * k : 3 * k + 3])
+
+        def load_x(k):
+            return (x_sb[k][:], x_planes[k // PACK, k % PACK])
+
+        loads = [load_c(0), (wt_raw[:].bitcast(I32), wt_words.bitcast(I32).rearrange("a p n -> p a n"))]
+        loads.extend(small[0:2] + [load_c(1)] + small[2:4] + [(offsets[:], offs), (wgt_sb[:], wgt)])
+        loads.extend(small[4:6] + [load_x(0)] + small[6:8])
+        loads.append((wx_raw[:], wx_words[0].rearrange("p n i -> p (n i)").bitcast(I32)))
+        loads.extend([load_c(2), load_x(1), (bias[:], b.rearrange("(p t) -> p t", t=PACK))])
+        loads.extend(load_x(k) for k in range(2, 2 * PACK))
         for dst, src in loads:
             nc.sync.dma_start(dst, src)
 
@@ -322,7 +318,9 @@ def tile_list_biasP_kernel(
         xq0 = {}
 
         def first_pass(u):
-            codes, scales = quantize(xb0[u][:], f"xq0_{u}")
+            codes = placed([P, 2 * W], U32, f"xq0_codes{u}", 2 + 2 * u)
+            scales = held([P, 2 * W], U8, f"xq0_scales{u}")
+            quantize_into((codes, scales), 0, xb0[u][:])
             for j0 in range(u * 2 * W, (u + 1) * 2 * W, SUB):
                 xq0[j0] = (codes, scales, j0 - u * 2 * W)
             for n in range(len(WIDTHS)):
@@ -336,7 +334,7 @@ def tile_list_biasP_kernel(
         stage = held([P, PACK * J], F32, "stage")
         picked1 = stage[:].rearrange("p (t j) -> p t j", t=PACK)
         xb1 = {
-            0: stage[:, 2 * J + 2 * W : 3 * J].bitcast(BF16),
+            0: stage[:, 2 * W : J].bitcast(BF16),
             1: stage[:, J + 2 * W : 2 * J].bitcast(BF16),
         }
         for n in range(2, len(WIDTHS)):
@@ -378,22 +376,22 @@ def tile_list_biasP_kernel(
             nc.vector.quantize_mx(out=y_codes[:].bitcast(FP8X4), scales=y_scales[:, cols], in_=yb[n][:])
             nc.sync.dma_start(out_words[:, cols], y_codes[:].bitcast(I32))
 
-        pick(0, 0, J)
+        pick(0, 0, 2 * W)
+        pick(1, 0, 2 * W)
+        pick(2, 0, J)
         first_pass(0)
         second_tier(1)
         for n in range(2, len(WIDTHS)):
             add_second_tier(n)
-        pick(1, 0, 2 * W)
-        first_pass(1)
-        pick(2, 0, 2 * W)
         pick(3, 0, W)
         pick(3, W, 2 * W)
         pick(3, 2 * W, J)
         round_x(0)
         round_x(1)
         close_sums(0)
+        first_pass(1)
         add_bias(0)
-        pick(2, 2 * W, J)
+        pick(0, 2 * W, J)
         close_sums(1)
         add_bias(1)
         pick(1, 2 * W, 3 * W)

@@ -26,7 +26,6 @@ WIDTHS = [256, 256, 256, 128, 128]
 STARTS = [sum(WIDTHS[:n]) for n in range(len(WIDTHS))]
 C_LOADS = [256, 256, 512]
 Y_ROUND_ON_SCALAR = (0,)
-X_ROUND_ON_VECTOR = (2, 3, 4)
 IN_PSUM = (2, 3)
 
 
@@ -337,16 +336,23 @@ def tile_list_biasP_kernel(
             0: stage[:, 2 * W : J].bitcast(BF16),
             1: stage[:, J + 2 * W : 2 * J].bitcast(BF16),
         }
+        xb1_late = held([P, PACK * 2 * W], BF16, "xb1_late")
         for n in range(2, len(WIDTHS)):
-            xb1[n] = held([P, PACK * WIDTHS[n]], BF16, f"xb1_{n}")[:]
+            first = PACK * (STARTS[n] - 2 * W)
+            xb1[n] = xb1_late[:, first : first + PACK * WIDTHS[n]]
         y = [held([P, PACK, W], F32, f"y{h}") for h in range(QUARTERS)]
         yb = [held([P, PACK * W], BF16, f"yb{h}") for h in range(QUARTERS)]
 
         def pick(i, j0, j1):
             gather(picked1[:, i, j0:j1], PACK + i, j0, j1)
 
-        def round_x(n):
-            weave(xb1[n], picked1[:, :, STARTS[n] : STARTS[n] + WIDTHS[n]], n in X_ROUND_ON_VECTOR)
+        def round_pair(dst, t0, j0, on_vector):
+            out = woven(dst)[:, :, t0 : t0 + 2, :]
+            src = planar(picked1[:, t0 : t0 + 2, j0 : j0 + dst.shape[1] // PACK])
+            if on_vector:
+                nc.vector.tensor_copy(out=out, in_=src)
+            else:
+                nc.scalar.activation(out=out, in_=src, func=ACT.Identity)
 
         def close_sums(n):
             per_bank = BANK // WIDTHS[n]
@@ -360,9 +366,9 @@ def tile_list_biasP_kernel(
             for t in range(PACK):
                 dst = y[h][:, t, first : first + WIDTHS[n]]
                 nc.scalar.activation(out=dst, in_=sum_of(n, t), func=ACT.Identity, bias=bias[:, t : t + 1])
-                if n == 0 and t % 2 == 1:
-                    nc.sync.dma_start(out_rows[:, t - 1 : t + 1, 0:W], y[0][:, t - 1 : t + 1, :])
-            if n > 0 and first + WIDTHS[n] == W:
+                if WIDTHS[n] == W and t % 2 == 1:
+                    nc.sync.dma_start(out_rows[:, t - 1 : t + 1, h * W : (h + 1) * W], y[h][:, t - 1 : t + 1, :])
+            if first > 0:
                 nc.sync.dma_start(out_rows[:, :, h * W : (h + 1) * W], y[h][:])
 
         def round_y(n):
@@ -378,6 +384,8 @@ def tile_list_biasP_kernel(
 
         pick(0, 0, 2 * W)
         pick(1, 0, 2 * W)
+        round_pair(xb1[0], 0, 0, False)
+        round_pair(xb1[1], 0, W, False)
         pick(2, 0, J)
         first_pass(0)
         second_tier(1)
@@ -386,8 +394,9 @@ def tile_list_biasP_kernel(
         pick(3, 0, W)
         pick(3, W, 2 * W)
         pick(3, 2 * W, J)
-        round_x(0)
-        round_x(1)
+        round_pair(xb1[0], 2, 0, False)
+        round_pair(xb1[1], 2, W, False)
+        round_pair(xb1_late[:], 2, 2 * W, False)
         close_sums(0)
         first_pass(1)
         add_bias(0)
@@ -395,11 +404,10 @@ def tile_list_biasP_kernel(
         close_sums(1)
         add_bias(1)
         pick(1, 2 * W, 3 * W)
-        round_x(2)
+        round_pair(xb1[2], 0, STARTS[2], True)
         pick(1, 3 * W, J)
         close_sums(2)
-        round_x(3)
-        round_x(4)
+        round_pair(xb1_late[:, PACK * W :], 0, STARTS[3], True)
         close_sums(3)
         close_sums(4)
         for n in range(2, len(WIDTHS)):

@@ -216,7 +216,7 @@ def tile_list_biasP_kernel(
             )
 
         def second_tier(h):
-            codes = placed([P, 2 * W], U32, "cr_late", 0) if h else held([P, 2 * W], U32, "cr_early")
+            codes = placed([P, 2 * W], U32, "cr_late", 8) if h else held([P, 2 * W], U32, "cr_early")
             cr[h] = (codes, held([P, 2 * W], U8, f"cr_scales{h}"))
             quantize_into(cr[h], 0, rb[h][:])
 
@@ -310,18 +310,21 @@ def tile_list_biasP_kernel(
             cuts = [0] + ([J // 2] if k == PACK - 1 else []) + [J]
             for j0, j1 in zip(cuts, cuts[1:]):
                 gather(picked0[:, k, j0:j1], k, j0, j1)
-        xb0 = [held([P, 2 * PACK * W], BF16, f"xb0_{u}") for u in range(2)]
+        stage = held([P, PACK * J], F32, "stage")
+        xb0 = [held([P, 2 * PACK * W], BF16, "xb0_first")[:], stage[:, 0:J].bitcast(BF16)]
         for u in range(2):
-            weave(xb0[u][:], picked0[:, :, u * 2 * W : (u + 1) * 2 * W], False)
+            weave(xb0[u], picked0[:, :, u * 2 * W : (u + 1) * 2 * W], False)
 
         xq0 = {}
 
         def first_pass(u):
-            codes = placed([P, 2 * W], U32, f"xq0_codes{u}", 2 + 2 * u)
+            codes = placed([P, 2 * W], U32, f"xq0_codes{u}", 10 if u else 0)
             scales = held([P, 2 * W], U8, f"xq0_scales{u}")
-            quantize_into((codes, scales), 0, xb0[u][:])
+            quantize_into((codes, scales), 0, xb0[u])
             for j0 in range(u * 2 * W, (u + 1) * 2 * W, SUB):
                 xq0[j0] = (codes, scales, j0 - u * 2 * W)
+
+        def add_first_pass(u):
             for n in range(len(WIDTHS)):
                 if STARTS[n] // (2 * W) == u:
                     for t in range(PACK):
@@ -330,10 +333,10 @@ def tile_list_biasP_kernel(
         out_rows = out_0.rearrange("(p t) j -> p t j", t=PACK)
         out_words = out_1[0].rearrange("p j i -> p (j i)").bitcast(I32)
         y_scales = held([P, J], U8, "y_scales")
-        stage = held([P, PACK * J], F32, "stage")
+        first_pair = held([P, 2, 2 * W], F32, "first_pair")
         picked1 = stage[:].rearrange("p (t j) -> p t j", t=PACK)
         xb1 = {
-            0: stage[:, 2 * W : J].bitcast(BF16),
+            0: placed([P, PACK * W], BF16, "xb1_first", 9)[:],
             1: stage[:, J + 2 * W : 2 * J].bitcast(BF16),
         }
         xb1_late = held([P, PACK * 2 * W], BF16, "xb1_late")
@@ -348,7 +351,8 @@ def tile_list_biasP_kernel(
 
         def round_pair(dst, t0, j0, on_vector):
             out = woven(dst)[:, :, t0 : t0 + 2, :]
-            src = planar(picked1[:, t0 : t0 + 2, j0 : j0 + dst.shape[1] // PACK])
+            pair = first_pair[:] if t0 == 0 and j0 < 2 * W else picked1[:, t0 : t0 + 2, :]
+            src = planar(pair[:, :, j0 : j0 + dst.shape[1] // PACK])
             if on_vector:
                 nc.vector.tensor_copy(out=out, in_=src)
             else:
@@ -382,15 +386,13 @@ def tile_list_biasP_kernel(
             nc.vector.quantize_mx(out=y_codes[:].bitcast(FP8X4), scales=y_scales[:, cols], in_=yb[n][:])
             nc.sync.dma_start(out_words[:, cols], y_codes[:].bitcast(I32))
 
-        pick(0, 0, 2 * W)
-        pick(1, 0, 2 * W)
+        for i in range(2):
+            gather(first_pair[:, i, :], PACK + i, 0, 2 * W)
         round_pair(xb1[0], 0, 0, False)
         round_pair(xb1[1], 0, W, False)
         pick(2, 0, J)
         first_pass(0)
-        second_tier(1)
-        for n in range(2, len(WIDTHS)):
-            add_second_tier(n)
+        add_first_pass(0)
         pick(3, 0, W)
         pick(3, W, 2 * W)
         pick(3, 2 * W, J)
@@ -399,21 +401,27 @@ def tile_list_biasP_kernel(
         round_pair(xb1_late[:], 2, 2 * W, False)
         close_sums(0)
         first_pass(1)
-        add_bias(0)
-        pick(0, 2 * W, J)
         close_sums(1)
+        second_tier(1)
+        add_first_pass(1)
+        for n in range(2, len(WIDTHS)):
+            add_second_tier(n)
+        add_bias(0)
         add_bias(1)
+        round_y(0)
+        pick(0, 2 * W, 3 * W)
         pick(1, 2 * W, 3 * W)
         round_pair(xb1[2], 0, STARTS[2], True)
-        pick(1, 3 * W, J)
+        pick(0, 3 * W, J)
         close_sums(2)
+        pick(1, 3 * W, J)
         round_pair(xb1_late[:, PACK * W :], 0, STARTS[3], True)
         close_sums(3)
         close_sums(4)
         for n in range(2, len(WIDTHS)):
             add_bias(n)
         for step in range(len(WIDTHS) + 1):
-            if step < len(WIDTHS):
+            if 1 <= step < len(WIDTHS):
                 round_y(step)
             if step in (1, 2, 3, 5):
                 hand_on(min(step - 1, QUARTERS - 1))

@@ -76,7 +76,8 @@ def tile_list_biasP_kernel(
         sc_raw = held([P, 2, N], U8, "sc_raw")
         bias = held([P, PACK], F32, "bias")
         wgt_sb = held([P, J], F32, "wgt_sb")
-        x_sb = [placed([P, T], F32, f"x{k}", 0) if k == PACK + 2 else held([P, T], F32, f"x{k}") for k in range(2 * PACK)]
+        x_at = {PACK + 2: 0, PACK: 16}
+        x_sb = [placed([P, T], F32, f"x{k}", x_at[k]) if k in x_at else held([P, T], F32, f"x{k}") for k in range(2 * PACK)]
         c_sb = [held([P, PACK, w], F32, f"c{h}") for h, w in enumerate(C_LOADS)]
 
         eye = held([P, PACK * (L + 1)], BF16, "eye")
@@ -126,8 +127,9 @@ def tile_list_biasP_kernel(
         loads = [load_c(0), (wt_raw[:].bitcast(I32), wt_words.bitcast(I32).rearrange("a p n -> p a n"))]
         loads.extend(small[0:2] + [load_c(1)] + small[2:4] + [(offsets[:], offs), (wgt_sb[:], wgt)])
         loads.extend(small[4:6] + [load_x(0)] + small[6:8])
+        loads.extend([load_c(2), load_x(1)])
         loads.append((wx_raw[:], wx_words[0].rearrange("p n i -> p (n i)").bitcast(I32)))
-        loads.extend([load_c(2), load_x(1), (bias[:], b.rearrange("(p t) -> p t", t=PACK))])
+        loads.append((bias[:], b.rearrange("(p t) -> p t", t=PACK)))
         loads.extend(load_x(k) for k in range(2, 2 * PACK))
         for dst, src in loads:
             nc.sync.dma_start(dst, src)
@@ -144,10 +146,14 @@ def tile_list_biasP_kernel(
 
         def round_c(h):
             cb[h] = held([P, PACK * W], BF16, f"cb{h}")
-            weave(cb[h][:], c_cols(h * W, (h + 1) * W), h == 0)
+            width = SUB if h == 0 else W
+            for j0 in range(0, W, width):
+                weave(cb[h][:, PACK * j0 : PACK * (j0 + width)], c_cols(h * W + j0, h * W + j0 + width), h == 0)
 
         def first_tier(h):
-            quantize_into(cq, h * W, cb[h][:])
+            width = SUB if h == 0 else W
+            for j0 in range(0, W, width):
+                quantize_into(cq, h * W + j0, cb[h][:, PACK * j0 : PACK * (j0 + width)])
 
         def leftover(h):
             codes, scales = cq
@@ -216,7 +222,7 @@ def tile_list_biasP_kernel(
             )
 
         def second_tier(h):
-            codes = placed([P, 2 * W], U32, "cr_late", 8) if h else held([P, 2 * W], U32, "cr_early")
+            codes = placed([P, 2 * W], U32, "cr_late", 16) if h else held([P, 2 * W], U32, "cr_early")
             cr[h] = (codes, held([P, 2 * W], U8, f"cr_scales{h}"))
             quantize_into(cr[h], 0, rb[h][:])
 
@@ -307,9 +313,7 @@ def tile_list_biasP_kernel(
 
         picked0 = held([P, PACK, J], F32, "picked0")
         for k in range(PACK):
-            cuts = [0] + ([J // 2] if k == PACK - 1 else []) + [J]
-            for j0, j1 in zip(cuts, cuts[1:]):
-                gather(picked0[:, k, j0:j1], k, j0, j1)
+            gather(picked0[:, k, :], k, 0, J)
         stage = held([P, PACK * J], F32, "stage")
         xb0 = [held([P, 2 * PACK * W], BF16, "xb0_first")[:], stage[:, 0:J].bitcast(BF16)]
         for u in range(2):
@@ -402,29 +406,33 @@ def tile_list_biasP_kernel(
         close_sums(0)
         first_pass(1)
         close_sums(1)
-        second_tier(1)
         add_first_pass(1)
-        for n in range(2, len(WIDTHS)):
-            add_second_tier(n)
         add_bias(0)
         add_bias(1)
         round_y(0)
-        pick(0, 2 * W, 3 * W)
+        pick(0, 2 * W, J)
         pick(1, 2 * W, 3 * W)
+        second_tier(1)
+        for n in range(2, len(WIDTHS)):
+            add_second_tier(n)
         round_pair(xb1[2], 0, STARTS[2], True)
-        pick(0, 3 * W, J)
+        pick(1, STARTS[3], STARTS[4])
         close_sums(2)
-        pick(1, 3 * W, J)
-        round_pair(xb1_late[:, PACK * W :], 0, STARTS[3], True)
+        pick(1, STARTS[4], J)
+        round_pair(xb1[3], 0, STARTS[3], True)
+        round_pair(xb1[4], 0, STARTS[4], True)
         close_sums(3)
         close_sums(4)
         for n in range(2, len(WIDTHS)):
             add_bias(n)
-        for step in range(len(WIDTHS) + 1):
-            if 1 <= step < len(WIDTHS):
-                round_y(step)
-            if step in (1, 2, 3, 5):
-                hand_on(min(step - 1, QUARTERS - 1))
+        round_y(1)
+        hand_on(0)
+        round_y(2)
+        hand_on(1)
+        round_y(3)
+        round_y(4)
+        hand_on(2)
+        hand_on(3)
         for Q in range(4):
             (nc.sync if Q % 2 == 0 else nc.scalar).dma_start(
                 out_2[0, 4 * Q : 4 * Q + 4, :].bitcast(I32), y_scales[32 * Q : 32 * Q + 4, :].bitcast(I32)

@@ -25,7 +25,7 @@ SUB = 128
 WIDTHS = [256, 256, 256, 128, 128]
 STARTS = [sum(WIDTHS[:n]) for n in range(len(WIDTHS))]
 C_LOADS = [256, 256, 512]
-Y_ROUND_ON_SCALAR = (0,)
+Y_ROUND_ON_SCALAR = (0, 1)
 IN_PSUM = (2, 3)
 
 
@@ -76,7 +76,7 @@ def tile_list_biasP_kernel(
         sc_raw = held([P, 2, N], U8, "sc_raw")
         bias = held([P, PACK], F32, "bias")
         wgt_sb = held([P, J], F32, "wgt_sb")
-        x_at = {PACK + 2: 0, PACK: 16}
+        x_at = {PACK + 2: 0, PACK + 3: 8}
         x_sb = [placed([P, T], F32, f"x{k}", x_at[k]) if k in x_at else held([P, T], F32, f"x{k}") for k in range(2 * PACK)]
         c_sb = [held([P, PACK, w], F32, f"c{h}") for h, w in enumerate(C_LOADS)]
 
@@ -222,7 +222,7 @@ def tile_list_biasP_kernel(
             )
 
         def second_tier(h):
-            codes = placed([P, 2 * W], U32, "cr_late", 16) if h else held([P, 2 * W], U32, "cr_early")
+            codes = placed([P, 2 * W], U32, "cr_late", 8) if h else held([P, 2 * W], U32, "cr_early")
             cr[h] = (codes, held([P, 2 * W], U8, f"cr_scales{h}"))
             quantize_into(cr[h], 0, rb[h][:])
 
@@ -314,8 +314,7 @@ def tile_list_biasP_kernel(
         picked0 = held([P, PACK, J], F32, "picked0")
         for k in range(PACK):
             gather(picked0[:, k, :], k, 0, J)
-        stage = held([P, PACK * J], F32, "stage")
-        xb0 = [held([P, 2 * PACK * W], BF16, "xb0_first")[:], stage[:, 0:J].bitcast(BF16)]
+        xb0 = [held([P, 2 * PACK * W], BF16, f"xb0_{u}")[:] for u in range(2)]
         for u in range(2):
             weave(xb0[u], picked0[:, :, u * 2 * W : (u + 1) * 2 * W], False)
 
@@ -337,12 +336,9 @@ def tile_list_biasP_kernel(
         out_rows = out_0.rearrange("(p t) j -> p t j", t=PACK)
         out_words = out_1[0].rearrange("p j i -> p (j i)").bitcast(I32)
         y_scales = held([P, J], U8, "y_scales")
-        first_pair = held([P, 2, 2 * W], F32, "first_pair")
-        picked1 = stage[:].rearrange("p (t j) -> p t j", t=PACK)
-        xb1 = {
-            0: placed([P, PACK * W], BF16, "xb1_first", 9)[:],
-            1: stage[:, J + 2 * W : 2 * J].bitcast(BF16),
-        }
+        stage = held([P, PACK * J + W], F32, "stage")
+        picked1 = stage[:, 0 : PACK * J].rearrange("p (t j) -> p t j", t=PACK)
+        xb1 = {0: stage[:, PACK * J - W :].bitcast(BF16), 1: stage[:, J + 2 * W : 2 * J].bitcast(BF16)}
         xb1_late = held([P, PACK * 2 * W], BF16, "xb1_late")
         for n in range(2, len(WIDTHS)):
             first = PACK * (STARTS[n] - 2 * W)
@@ -355,8 +351,7 @@ def tile_list_biasP_kernel(
 
         def round_pair(dst, t0, j0, on_vector):
             out = woven(dst)[:, :, t0 : t0 + 2, :]
-            pair = first_pair[:] if t0 == 0 and j0 < 2 * W else picked1[:, t0 : t0 + 2, :]
-            src = planar(pair[:, :, j0 : j0 + dst.shape[1] // PACK])
+            src = planar(picked1[:, t0 : t0 + 2, j0 : j0 + dst.shape[1] // PACK])
             if on_vector:
                 nc.vector.tensor_copy(out=out, in_=src)
             else:
@@ -376,13 +371,24 @@ def tile_list_biasP_kernel(
                 nc.scalar.activation(out=dst, in_=sum_of(n, t), func=ACT.Identity, bias=bias[:, t : t + 1])
                 if WIDTHS[n] == W and t % 2 == 1:
                     nc.sync.dma_start(out_rows[:, t - 1 : t + 1, h * W : (h + 1) * W], y[h][:, t - 1 : t + 1, :])
-            if first > 0:
-                nc.sync.dma_start(out_rows[:, :, h * W : (h + 1) * W], y[h][:])
+            if WIDTHS[n] < W:
+                cols = slice(STARTS[n], STARTS[n] + WIDTHS[n])
+                nc.sync.dma_start(out_rows[:, :, cols], y[h][:, :, first : first + WIDTHS[n]])
 
         def round_y(n):
             h, first = divmod(STARTS[n], W)
             dst = yb[h][:, PACK * first : PACK * (first + WIDTHS[n])]
             weave(dst, y[h][:, :, first : first + WIDTHS[n]], n not in Y_ROUND_ON_SCALAR)
+
+        def round_sums(n):
+            h, first = divmod(STARTS[n], W)
+            dst = yb[h][:, PACK * first : PACK * (first + WIDTHS[n])]
+            nc.vector.tensor_tensor(
+                out=dst.rearrange("p (j t) -> p j t", t=PACK),
+                in0=banks[n, 0][:].rearrange("p t j -> p j t"),
+                in1=bias[:].unsqueeze(1).to_broadcast([P, WIDTHS[n], PACK]),
+                op=ALU.add,
+            )
 
         def hand_on(n):
             cols = slice(n * W, (n + 1) * W)
@@ -390,8 +396,8 @@ def tile_list_biasP_kernel(
             nc.vector.quantize_mx(out=y_codes[:].bitcast(FP8X4), scales=y_scales[:, cols], in_=yb[n][:])
             nc.sync.dma_start(out_words[:, cols], y_codes[:].bitcast(I32))
 
-        for i in range(2):
-            gather(first_pair[:, i, :], PACK + i, 0, 2 * W)
+        pick(0, 0, J)
+        pick(1, 0, 2 * W)
         round_pair(xb1[0], 0, 0, False)
         round_pair(xb1[1], 0, W, False)
         pick(2, 0, J)
@@ -399,38 +405,35 @@ def tile_list_biasP_kernel(
         add_first_pass(0)
         pick(3, 0, W)
         pick(3, W, 2 * W)
-        pick(3, 2 * W, J)
-        round_pair(xb1[0], 2, 0, False)
-        round_pair(xb1[1], 2, W, False)
-        round_pair(xb1_late[:], 2, 2 * W, False)
+        pick(3, 2 * W, 3 * W)
+        for h in range(3):
+            round_pair(xb1[h], 2, h * W, False)
         close_sums(0)
-        first_pass(1)
+        pick(3, 3 * W, J)
         close_sums(1)
+        first_pass(1)
+        second_tier(1)
         add_first_pass(1)
+        for n in range(2, len(WIDTHS)):
+            add_second_tier(n)
         add_bias(0)
         add_bias(1)
         round_y(0)
-        pick(0, 2 * W, J)
+        round_y(1)
         pick(1, 2 * W, 3 * W)
-        second_tier(1)
-        for n in range(2, len(WIDTHS)):
-            add_second_tier(n)
         round_pair(xb1[2], 0, STARTS[2], True)
-        pick(1, STARTS[3], STARTS[4])
+        pick(1, 3 * W, J)
         close_sums(2)
-        pick(1, STARTS[4], J)
-        round_pair(xb1[3], 0, STARTS[3], True)
-        round_pair(xb1[4], 0, STARTS[4], True)
+        weave(xb1_late[:, PACK * W :], picked1[:, :, 3 * W : J], True)
         close_sums(3)
         close_sums(4)
+        round_sums(4)
         for n in range(2, len(WIDTHS)):
             add_bias(n)
-        round_y(1)
         hand_on(0)
-        round_y(2)
         hand_on(1)
+        round_y(2)
         round_y(3)
-        round_y(4)
         hand_on(2)
         hand_on(3)
         for Q in range(4):

@@ -245,14 +245,14 @@ def tile_list_biasP_kernel(
                 second_tier(0)
 
         wt_d = held([P, 2 * 2 * N], U8, "wt_d")
-        nc.vector.tensor_copy(
+        nc.scalar.copy(
             out=wt_d[:].bitcast(U16).rearrange("p (a t q i) -> p a q t i", a=2, t=PACK, i=8),
             in_=wt_raw[:].bitcast(U16).rearrange("p a (q i t) -> p a q t i", t=PACK, i=8),
         )
         wx_d = held([P, N], I32, "wx_d")
-        nc.vector.tensor_copy(
-            out=wx_d[:].rearrange("p (t q i) -> p q t i", t=PACK, i=4),
-            in_=wx_raw[:].rearrange("p (q i t) -> p q t i", t=PACK, i=4),
+        nc.scalar.copy(
+            out=wx_d[:].bitcast(U32).rearrange("p (t q i) -> p q t i", t=PACK, i=4),
+            in_=wx_raw[:].bitcast(U32).rearrange("p (q i t) -> p q t i", t=PACK, i=4),
         )
         sc_d = held([P, 2 * N], U8, "sc_d")
         nc.vector.tensor_copy(

@@ -44,9 +44,6 @@ def tile_list_biasP_kernel(
         def placed(shape, dtype, name, kib):
             return shared.tile(shape, dtype, name=name, align_bytes=64, offset=int(kib * 1024))
 
-        def operand(name):
-            return held([P, J], U32, name + "_codes"), held([P, J], U8, name + "_scales")
-
         def quantize_into(dst, j0, src):
             cols = slice(j0, j0 + src.shape[1] // PACK)
             nc.vector.quantize_mx(out=dst[0][:, cols].bitcast(FP8X4), scales=dst[1][:, cols], in_=src)
@@ -76,7 +73,7 @@ def tile_list_biasP_kernel(
         sc_raw = held([P, 2, N], U8, "sc_raw")
         bias = held([P, PACK], F32, "bias")
         wgt_sb = held([P, J], F32, "wgt_sb")
-        x_at = {PACK + 2: 0, PACK + 3: 8}
+        x_at = {0: 16, PACK: 0, PACK + 3: 8}
         x_sb = [placed([P, T], F32, f"x{k}", x_at[k]) if k in x_at else held([P, T], F32, f"x{k}") for k in range(2 * PACK)]
         c_sb = [held([P, PACK, w], F32, f"c{h}") for h, w in enumerate(C_LOADS)]
 
@@ -124,15 +121,31 @@ def tile_list_biasP_kernel(
         def load_x(k):
             return (x_sb[k][:], x_planes[k // PACK, k % PACK])
 
-        loads = [load_c(0), (wt_raw[:].bitcast(I32), wt_words.bitcast(I32).rearrange("a p n -> p a n"))]
-        loads.extend(small[0:2] + [load_c(1)] + small[2:4] + [(offsets[:], offs), (wgt_sb[:], wgt)])
-        loads.extend(small[4:6] + [load_x(0)] + small[6:8])
-        loads.extend([load_c(2), load_x(1)])
-        loads.append((wx_raw[:], wx_words[0].rearrange("p n i -> p (n i)").bitcast(I32)))
-        loads.append((bias[:], b.rearrange("(p t) -> p t", t=PACK)))
-        loads.extend(load_x(k) for k in range(2, 2 * PACK))
+        wgt_rows = held([P, P], F32, "wgt_rows")
+        nc.gpsimd.memset(wgt_rows[64:P, :], 0.0)
+        wt_load = (wt_raw[:].bitcast(I32), wt_words.bitcast(I32).rearrange("a p n -> p a n"))
+        wx_load = (wx_raw[:], wx_words[0].rearrange("p n i -> p (n i)").bitcast(I32))
+        bias_load = (bias[:], b.rearrange("(p t) -> p t", t=PACK))
+        loads = [(wgt_rows[0:64, :], wgt[0:P:16, :]), load_c(0), load_c(1), load_c(2), (offsets[:], offs), load_x(0)]
+        loads.extend(small[0:2] + [wt_load] + small[2:4] + [load_x(1)] + small[4:6] + [wx_load, load_x(2)])
+        loads.extend(small[6:8] + [load_x(3), bias_load])
+        loads.extend(load_x(k) for k in range(PACK, 2 * PACK))
         for dst, src in loads:
             nc.sync.dma_start(dst, src)
+
+        turned_rows = psum.tile([P, P], F32, name="turned_rows", tag="bank")
+        nc.tensor.transpose(turned_rows[:], wgt_rows[:], ident[:])
+        wgt_banks = []
+        for u in range(2):
+            spread = held([P, PACK, 8, 16], F32, f"spread{u}")
+            blocks = turned_rows[:, 0:64].rearrange("j (g b) -> j b g", b=8)[:, PACK * u : PACK * (u + 1), :]
+            nc.scalar.copy(out=spread[:], in_=blocks.unsqueeze(3).to_broadcast([P, PACK, 8, 16]))
+            wgt_banks.append(psum.tile([P, PACK, P], F32, name="wgt_bank", tag="bank"))
+            for v in range(PACK):
+                nc.tensor.transpose(wgt_banks[u][:, v, :], spread[:, v, :, :].rearrange("j g r -> j (g r)"), ident[:])
+
+        def take_wgt(u):
+            nc.scalar.copy(out=wgt_sb[:, u * BANK : (u + 1) * BANK], in_=wgt_banks[u][:].rearrange("p v j -> p (v j)"))
 
         def c_cols(j0, j1):
             h = max(u for u in range(len(C_LOADS)) if sum(C_LOADS[:u]) <= j0)
@@ -140,7 +153,8 @@ def tile_list_biasP_kernel(
             return c_sb[h][:, :, j0 - first : j1 - first]
 
         cb = {}
-        cq = operand("cq")
+        cq = [(held([P, W], U32, f"cq{h}"), held([P, W], U8, f"cq_scales{h}")) for h in range(QUARTERS - 1)]
+        cq.append((placed([P, W], U32, "cq_last", 16), held([P, W], U8, "cq_scales_last")))
         cr = {}
         rb = [held([P, 2 * PACK * W], BF16, f"rb{u}") for u in range(2)]
 
@@ -153,13 +167,13 @@ def tile_list_biasP_kernel(
         def first_tier(h):
             width = SUB if h == 0 else W
             for j0 in range(0, W, width):
-                quantize_into(cq, h * W + j0, cb[h][:, PACK * j0 : PACK * (j0 + width)])
+                quantize_into(cq[h], j0, cb[h][:, PACK * j0 : PACK * (j0 + width)])
 
         def leftover(h):
-            codes, scales = cq
+            codes, scales = cq[h]
             backs = []
             for s in range(W // SUB):
-                cols = slice(h * W + s * SUB, h * W + (s + 1) * SUB)
+                cols = slice(s * SUB, (s + 1) * SUB)
                 at = (h % 2 * W + s * SUB) * PACK
                 back = psum.tile([P, PACK, SUB], F32, name="back", tag="bank")
                 for t in range(PACK):
@@ -182,7 +196,19 @@ def tile_list_biasP_kernel(
                         op=ALU.subtract,
                     )
             if h in IN_PSUM:
+                turn_c(h)
                 leftover_in_psum(h, backs)
+
+        rests = {}
+
+        def turn_c(h):
+            for s in range(W // SUB):
+                rests[h, s] = psum.tile([P, PACK, P], F32, name="rest", tag="bank")
+                src = c_cols(h * W + s * SUB, h * W + (s + 1) * SUB)
+                for t in range(PACK):
+                    nc.tensor.matmul(
+                        rests[h, s][:, t, :], lhsT=src[:, t, :], rhs=ident[:], is_transpose=True, start=t == 0, stop=False
+                    )
 
         def leftover_in_psum(h, backs):
             minus = []
@@ -191,12 +217,7 @@ def tile_list_biasP_kernel(
                 nc.scalar.activation(out=minus[s][:], in_=back[:], func=ACT.Identity, scale=-1.0)
             pairs = []
             for s in range(W // SUB):
-                rest = psum.tile([P, PACK, P], F32, name="rest", tag="bank")
-                src = c_cols(h * W + s * SUB, h * W + (s + 1) * SUB)
-                for t in range(PACK):
-                    nc.tensor.matmul(
-                        rest[:, t, :], lhsT=src[:, t, :], rhs=ident[:], is_transpose=True, start=t == 0, stop=False
-                    )
+                rest = rests[h, s]
                 for t in range(PACK):
                     nc.tensor.matmul(
                         rest[:, t, :],
@@ -206,7 +227,10 @@ def tile_list_biasP_kernel(
                         start=False,
                         stop=t == PACK - 1,
                     )
-                pairs.append(held([P, 2, P, 2], BF16, f"pairs{h}_{s}"))
+                if (h, s) == (QUARTERS - 1, W // SUB - 1):
+                    pairs.append(placed([P, 2, P, 2], BF16, "pairs_last", 24))
+                else:
+                    pairs.append(held([P, 2, P, 2], BF16, f"pairs{h}_{s}"))
                 nc.scalar.activation(
                     out=pairs[s][:], in_=rest[:].rearrange("j (u e) p -> j u p e", e=2), func=ACT.Identity
                 )
@@ -234,12 +258,21 @@ def tile_list_biasP_kernel(
                 op=ALU.mult,
             )
 
-        for h in range(QUARTERS):
-            round_c(h)
+        round_c(0)
+        round_c(1)
+        take_wgt(0)
+        take_wgt(1)
+        picked0 = held([P, PACK, J], F32, "picked0")
         for h in range(QUARTERS + 2):
+            if h == 2:
+                leftover(1)
+                round_c(2)
+                round_c(3)
+            if h == QUARTERS - 1:
+                gather(picked0[:, 0, :], 0, 0, J)
             if h < QUARTERS:
                 first_tier(h)
-            if 1 <= h <= QUARTERS:
+            if 1 <= h <= QUARTERS and h != 2:
                 leftover(h - 1)
             if h == 3:
                 second_tier(0)
@@ -279,27 +312,26 @@ def tile_list_biasP_kernel(
             )
 
         def wt_pass(n, t, a, operand, last):
-            subs = WIDTHS[n] // SUB
-            for s in range(subs):
-                codes, scales, first = operand[STARTS[n] + s * SUB]
-                cols = slice(first, first + SUB)
-                nc.tensor.matmul_mx(
-                    out=sum_of(n, t)[:, s * SUB : (s + 1) * SUB],
-                    lhsT=wt_d[:, (a * N + t * P) * 2 : (a * N + (t + 1) * P) * 2].bitcast(FP4X4),
-                    lhsT_scale=sc_d[:, a * N + t * P : a * N + (t + 1) * P],
-                    rhs=codes[:, cols].bitcast(FP8X4),
-                    rhs_scale=scales[:, cols],
-                    start=False,
-                    stop=last and s == subs - 1,
-                )
+            codes, scales, first = operand[STARTS[n]]
+            cols = slice(first, first + WIDTHS[n])
+            nc.tensor.matmul_mx(
+                out=sum_of(n, t),
+                lhsT=wt_d[:, (a * N + t * P) * 2 : (a * N + (t + 1) * P) * 2].bitcast(FP4X4),
+                lhsT_scale=sc_d[:, a * N + t * P : a * N + (t + 1) * P],
+                rhs=codes[:, cols].bitcast(FP8X4),
+                rhs_scale=scales[:, cols],
+                start=False,
+                stop=last,
+            )
 
         def open_sums(n):
-            cols = slice(STARTS[n], STARTS[n] + WIDTHS[n])
+            h, first = divmod(STARTS[n], W)
+            cols = slice(first, first + WIDTHS[n])
             per_bank = BANK // WIDTHS[n]
             for u in range(PACK // per_bank):
                 banks[n, u] = psum.tile([P, per_bank, WIDTHS[n]], F32, name="acc", tag="bank")
             for t in range(PACK):
-                wx_pass(n, t, cq, cols, t % per_bank == 0)
+                wx_pass(n, t, cq[h], cols, t % per_bank == 0)
 
         def add_second_tier(n):
             half, first = divmod(STARTS[n], 2 * W)
@@ -311,12 +343,16 @@ def tile_list_biasP_kernel(
             if STARTS[n] < 2 * W:
                 add_second_tier(n)
 
-        picked0 = held([P, PACK, J], F32, "picked0")
-        for k in range(PACK):
+        for k in range(1, PACK):
             gather(picked0[:, k, :], k, 0, J)
-        xb0 = [held([P, 2 * PACK * W], BF16, f"xb0_{u}")[:] for u in range(2)]
-        for u in range(2):
-            weave(xb0[u], picked0[:, :, u * 2 * W : (u + 1) * 2 * W], False)
+        xb0 = [placed([P, 2 * PACK * W], BF16, f"xb0_{u}", 24 + 4 * u)[:] for u in range(2)]
+        for t0 in (0, 2):
+            nc.scalar.activation(
+                out=woven(xb0[0])[:, :, t0 : t0 + 2, :],
+                in_=planar(picked0[:, t0 : t0 + 2, 0 : 2 * W]),
+                func=ACT.Identity,
+            )
+        weave(xb0[1], picked0[:, :, 2 * W : J], False)
 
         xq0 = {}
 
@@ -400,9 +436,9 @@ def tile_list_biasP_kernel(
         pick(1, 0, 2 * W)
         round_pair(xb1[0], 0, 0, False)
         round_pair(xb1[1], 0, W, False)
-        pick(2, 0, J)
         first_pass(0)
         add_first_pass(0)
+        pick(2, 0, J)
         pick(3, 0, W)
         pick(3, W, 2 * W)
         pick(3, 2 * W, 3 * W)

@@ -22,6 +22,7 @@ BANK = 512
 W = 256
 QUARTERS = J // W
 SUB = 128
+PITCH = J + 3 * W
 WIDTHS = [256, 256, 256, 128, 128]
 STARTS = [sum(WIDTHS[:n]) for n in range(len(WIDTHS))]
 C_LOADS = [256, 256, 512]
@@ -156,13 +157,14 @@ def tile_list_biasP_kernel(
         cq = [(held([P, W], U32, f"cq{h}"), held([P, W], U8, f"cq_scales{h}")) for h in range(QUARTERS - 1)]
         cq.append((placed([P, W], U32, "cq_last", 16), held([P, W], U8, "cq_scales_last")))
         cr = {}
-        rb = [held([P, 2 * PACK * W], BF16, f"rb{u}") for u in range(2)]
+        stage = held([P, PACK * PITCH], F32, "stage")
+        rb = [held([P, 2 * PACK * W], BF16, "rb_early")[:], stage[:, 2 * PITCH + 3 * W : 3 * PITCH].bitcast(BF16)]
 
         def round_c(h):
             cb[h] = held([P, PACK * W], BF16, f"cb{h}")
             width = SUB if h == 0 else W
             for j0 in range(0, W, width):
-                weave(cb[h][:, PACK * j0 : PACK * (j0 + width)], c_cols(h * W + j0, h * W + j0 + width), h == 0)
+                weave(cb[h][:, PACK * j0 : PACK * (j0 + width)], c_cols(h * W + j0, h * W + j0 + width), h <= 1)
 
         def first_tier(h):
             width = SUB if h == 0 else W
@@ -248,7 +250,7 @@ def tile_list_biasP_kernel(
         def second_tier(h):
             codes = placed([P, 2 * W], U32, "cr_late", 8) if h else held([P, 2 * W], U32, "cr_early")
             cr[h] = (codes, held([P, 2 * W], U8, f"cr_scales{h}"))
-            quantize_into(cr[h], 0, rb[h][:])
+            quantize_into(cr[h], 0, rb[h])
 
         def gather(dst, k, j0, j1):
             nc.vector.tensor_tensor(
@@ -372,9 +374,8 @@ def tile_list_biasP_kernel(
         out_rows = out_0.rearrange("(p t) j -> p t j", t=PACK)
         out_words = out_1[0].rearrange("p j i -> p (j i)").bitcast(I32)
         y_scales = held([P, J], U8, "y_scales")
-        stage = held([P, PACK * J + W], F32, "stage")
-        picked1 = stage[:, 0 : PACK * J].rearrange("p (t j) -> p t j", t=PACK)
-        xb1 = {0: stage[:, PACK * J - W :].bitcast(BF16), 1: stage[:, J + 2 * W : 2 * J].bitcast(BF16)}
+        picked1 = stage[:].rearrange("p (t j) -> p t j", t=PACK)
+        xb1 = {0: picked1[:, 3, 3 * W : J + W].bitcast(BF16), 1: picked1[:, 1, 2 * W : J].bitcast(BF16)}
         xb1_late = held([P, PACK * 2 * W], BF16, "xb1_late")
         for n in range(2, len(WIDTHS)):
             first = PACK * (STARTS[n] - 2 * W)
@@ -438,7 +439,7 @@ def tile_list_biasP_kernel(
         round_pair(xb1[1], 0, W, False)
         first_pass(0)
         add_first_pass(0)
-        pick(2, 0, J)
+        pick(2, 0, 3 * W)
         pick(3, 0, W)
         pick(3, W, 2 * W)
         pick(3, 2 * W, 3 * W)
@@ -459,6 +460,7 @@ def tile_list_biasP_kernel(
         pick(1, 2 * W, 3 * W)
         round_pair(xb1[2], 0, STARTS[2], True)
         pick(1, 3 * W, J)
+        pick(2, 3 * W, J)
         close_sums(2)
         weave(xb1_late[:, PACK * W :], picked1[:, :, 3 * W : J], True)
         close_sums(3)

@@ -215,7 +215,10 @@ def tile_list_biasP_kernel(
         def leftover_in_psum(h, backs):
             minus = []
             for s, back in enumerate(backs):
-                minus.append(held([P, PACK, SUB], F32, f"minus{h}_{s}"))
+                if (h, s) == (QUARTERS - 1, 0):
+                    minus.append(placed([P, PACK, SUB], F32, "minus_last", 24))
+                else:
+                    minus.append(held([P, PACK, SUB], F32, f"minus{h}_{s}"))
                 nc.scalar.activation(out=minus[s][:], in_=back[:], func=ACT.Identity, scale=-1.0)
             pairs = []
             for s in range(W // SUB):
@@ -229,10 +232,7 @@ def tile_list_biasP_kernel(
                         start=False,
                         stop=t == PACK - 1,
                     )
-                if (h, s) == (QUARTERS - 1, W // SUB - 1):
-                    pairs.append(placed([P, 2, P, 2], BF16, "pairs_last", 24))
-                else:
-                    pairs.append(held([P, 2, P, 2], BF16, f"pairs{h}_{s}"))
+                pairs.append(held([P, 2, P, 2], BF16, f"pairs{h}_{s}"))
                 nc.scalar.activation(
                     out=pairs[s][:], in_=rest[:].rearrange("j (u e) p -> j u p e", e=2), func=ACT.Identity
                 )
@@ -401,16 +401,15 @@ def tile_list_biasP_kernel(
             for t in range(PACK):
                 wt_pass(n, t, 1, xq1, t % per_bank == per_bank - 1)
 
-        def add_bias(n):
-            h, first = divmod(STARTS[n], W)
-            for t in range(PACK):
-                dst = y[h][:, t, first : first + WIDTHS[n]]
-                nc.scalar.activation(out=dst, in_=sum_of(n, t), func=ACT.Identity, bias=bias[:, t : t + 1])
-                if WIDTHS[n] == W and t % 2 == 1:
-                    nc.sync.dma_start(out_rows[:, t - 1 : t + 1, h * W : (h + 1) * W], y[h][:, t - 1 : t + 1, :])
-            if WIDTHS[n] < W:
-                cols = slice(STARTS[n], STARTS[n] + WIDTHS[n])
-                nc.sync.dma_start(out_rows[:, :, cols], y[h][:, :, first : first + WIDTHS[n]])
+        def add_bias(h):
+            chunks = [n for n in range(len(WIDTHS)) if STARTS[n] // W == h]
+            for t0 in (0, 2):
+                for n in chunks:
+                    first = STARTS[n] - h * W
+                    for t in (t0, t0 + 1):
+                        dst = y[h][:, t, first : first + WIDTHS[n]]
+                        nc.scalar.activation(out=dst, in_=sum_of(n, t), func=ACT.Identity, bias=bias[:, t : t + 1])
+                nc.sync.dma_start(out_rows[:, t0 : t0 + 2, h * W : (h + 1) * W], y[h][:, t0 : t0 + 2, :])
 
         def round_y(n):
             h, first = divmod(STARTS[n], W)
@@ -466,8 +465,8 @@ def tile_list_biasP_kernel(
         close_sums(3)
         close_sums(4)
         round_sums(4)
-        for n in range(2, len(WIDTHS)):
-            add_bias(n)
+        add_bias(2)
+        add_bias(3)
         hand_on(0)
         hand_on(1)
         round_y(2)

@@ -128,8 +128,8 @@ def tile_list_biasP_kernel(
         wx_load = (wx_raw[:], wx_words[0].rearrange("p n i -> p (n i)").bitcast(I32))
         bias_load = (bias[:], b.rearrange("(p t) -> p t", t=PACK))
         loads = [(wgt_rows[0:64, :], wgt[0:P:16, :]), load_c(0), load_c(1), load_c(2), (offsets[:], offs), load_x(0)]
-        loads.extend(small[0:2] + [wt_load] + small[2:4] + [load_x(1)] + small[4:6] + [wx_load, load_x(2)])
-        loads.extend(small[6:8] + [load_x(3), bias_load])
+        loads.extend(small[0:2] + [load_x(1)] + small[2:4] + [load_x(2)] + small[4:6] + [wt_load, load_x(3)])
+        loads.extend(small[6:8] + [wx_load, bias_load])
         loads.extend(load_x(k) for k in range(PACK, 2 * PACK))
         for dst, src in loads:
             nc.sync.dma_start(dst, src)
@@ -162,12 +162,12 @@ def tile_list_biasP_kernel(
 
         def round_c(h):
             cb[h] = held([P, PACK * W], BF16, f"cb{h}")
-            width = SUB if h == 0 else W
+            width = SUB if h <= 1 else W
             for j0 in range(0, W, width):
-                weave(cb[h][:, PACK * j0 : PACK * (j0 + width)], c_cols(h * W + j0, h * W + j0 + width), h <= 1)
+                weave(cb[h][:, PACK * j0 : PACK * (j0 + width)], c_cols(h * W + j0, h * W + j0 + width), h == 0)
 
         def first_tier(h):
-            width = SUB if h == 0 else W
+            width = SUB if h <= 1 else W
             for j0 in range(0, W, width):
                 quantize_into(cq[h], j0, cb[h][:, PACK * j0 : PACK * (j0 + width)])
 

@@ -248,7 +248,7 @@ def tile_list_biasP_kernel(
             )
 
         def second_tier(h):
-            codes = placed([P, 2 * W], U32, "cr_late", 8) if h else held([P, 2 * W], U32, "cr_early")
+            codes = placed([P, 2 * W], U32, "cr_late", 2) if h else held([P, 2 * W], U32, "cr_early")
             cr[h] = (codes, held([P, 2 * W], U8, f"cr_scales{h}"))
             quantize_into(cr[h], 0, rb[h])
 
@@ -438,7 +438,10 @@ def tile_list_biasP_kernel(
         round_pair(xb1[1], 0, W, False)
         first_pass(0)
         add_first_pass(0)
-        pick(2, 0, 3 * W)
+        second_tier(1)
+        pick(2, 0, J)
+        for n in range(2, len(WIDTHS)):
+            add_second_tier(n)
         pick(3, 0, W)
         pick(3, W, 2 * W)
         pick(3, 2 * W, 3 * W)
@@ -448,18 +451,14 @@ def tile_list_biasP_kernel(
         pick(3, 3 * W, J)
         close_sums(1)
         first_pass(1)
-        second_tier(1)
         add_first_pass(1)
-        for n in range(2, len(WIDTHS)):
-            add_second_tier(n)
         add_bias(0)
         add_bias(1)
         round_y(0)
-        round_y(1)
+        weave(yb[1][:, 0 : PACK * SUB], y[1][:, :, 0:SUB], False)
         pick(1, 2 * W, 3 * W)
         round_pair(xb1[2], 0, STARTS[2], True)
         pick(1, 3 * W, J)
-        pick(2, 3 * W, J)
         close_sums(2)
         weave(xb1_late[:, PACK * W :], picked1[:, :, 3 * W : J], True)
         close_sums(3)
@@ -468,6 +467,7 @@ def tile_list_biasP_kernel(
         add_bias(2)
         add_bias(3)
         hand_on(0)
+        weave(yb[1][:, PACK * SUB :], y[1][:, :, SUB:W], True)
         hand_on(1)
         round_y(2)
         round_y(3)

@@ -22,12 +22,8 @@ BANK = 512
 W = 256
 QUARTERS = J // W
 SUB = 128
-PITCH = J + 3 * W
-WIDTHS = [256, 256, 256, 128, 128]
+WIDTHS = [W, W, W, SUB, SUB]
 STARTS = [sum(WIDTHS[:n]) for n in range(len(WIDTHS))]
-C_LOADS = [256, 256, 512]
-Y_ROUND_ON_SCALAR = (0, 1)
-IN_PSUM = (2, 3)
 
 
 def tile_list_biasP_kernel(
@@ -43,11 +39,7 @@ def tile_list_biasP_kernel(
             return keep.tile(shape, dtype, name=name, align_bytes=64)
 
         def placed(shape, dtype, name, kib):
-            return shared.tile(shape, dtype, name=name, align_bytes=64, offset=int(kib * 1024))
-
-        def quantize_into(dst, j0, src):
-            cols = slice(j0, j0 + src.shape[1] // PACK)
-            nc.vector.quantize_mx(out=dst[0][:, cols].bitcast(FP8X4), scales=dst[1][:, cols], in_=src)
+            return shared.tile(shape, dtype, name=name, align_bytes=64, offset=kib * 1024)
 
         def planar(t3):
             return t3.rearrange("p t (q i) -> p q t i", i=4)
@@ -55,18 +47,19 @@ def tile_list_biasP_kernel(
         def woven(t2):
             return t2.rearrange("p (q i t) -> p q t i", i=4, t=PACK)
 
-        def weave(dst, src, on_vector):
+        def weave(out, src, on_vector):
             if on_vector:
-                nc.vector.tensor_copy(out=woven(dst), in_=planar(src))
+                nc.vector.tensor_copy(out=out, in_=planar(src))
             else:
-                nc.scalar.activation(out=woven(dst), in_=planar(src), func=ACT.Identity)
+                nc.scalar.activation(out=out, in_=planar(src), func=ACT.Identity)
 
-        def quantize(src, name):
-            width = src.shape[1] // PACK
-            codes = held([P, width], U32, name + "_codes")
-            scales = held([P, width], U8, name + "_scales")
-            nc.vector.quantize_mx(out=codes[:].bitcast(FP8X4), scales=scales[:], in_=src)
-            return codes, scales
+        def operand(name, width, kib=None):
+            codes = held([P, width], U32, name) if kib is None else placed([P, width], U32, name, kib)
+            return codes, held([P, width], U8, name + "_scales")
+
+        def quantize(dst, first, src):
+            cols = slice(first, first + src.shape[1] // PACK)
+            nc.vector.quantize_mx(out=dst[0][:, cols].bitcast(FP8X4), scales=dst[1][:, cols], in_=src)
 
         offsets = held([P, J // 16], U16, "offsets")
         wt_raw = held([P, 2, 2 * N], U8, "wt_raw")
@@ -74,183 +67,156 @@ def tile_list_biasP_kernel(
         sc_raw = held([P, 2, N], U8, "sc_raw")
         bias = held([P, PACK], F32, "bias")
         wgt_sb = held([P, J], F32, "wgt_sb")
-        x_at = {0: 16, PACK: 0, PACK + 3: 8}
-        x_sb = [placed([P, T], F32, f"x{k}", x_at[k]) if k in x_at else held([P, T], F32, f"x{k}") for k in range(2 * PACK)]
-        c_sb = [held([P, PACK, w], F32, f"c{h}") for h, w in enumerate(C_LOADS)]
+        wgt_rows = held([P, P], F32, "wgt_rows")
+        x_sb = [held([P, T], F32, f"x{k}") for k in range(PACK)]
+        x_sb.extend(placed([P, T], F32, f"x{PACK + i}", 8 * i) for i in range(PACK))
+        c_sb = [held([P, PACK, W], F32, f"c{h}") for h in range(QUARTERS)]
 
         eye = held([P, PACK * (L + 1)], BF16, "eye")
         ones = held([P, P], F32, "ones")
         ramp = held([P, P], F32, "ramp")
         base = held([P, 1], F32, "base")
         turned = held([P, 32], F32, "turned")
+        ident = held([P, P], F32, "ident")
         nc.gpsimd.memset(eye[:].bitcast(I32), 0)
         nc.vector.memset(ones[:], 1.0)
         for Q in range(4):
             nc.vector.memset(base[32 * Q : 32 * Q + 32, :], float(32 * Q))
         nc.vector.tensor_tensor_scan(out=ramp[:], data0=ones[:], data1=ones[:], initial=0.0, op0=ALU.mult, op1=ALU.add)
         nc.vector.transpose(out=turned[:], in_=ramp[:, 0:32])
-        nc.vector.tensor_scalar(
-            out=eye[:].rearrange("p (t x) -> p t x", t=PACK)[:, :, 0:L:PACK],
-            in0=ramp[:].unsqueeze(1).to_broadcast([P, PACK, P]),
-            scalar1=base[:],
-            scalar2=turned[:, 0:1],
-            op0=ALU.subtract,
-            op1=ALU.is_equal,
-        )
-        ident = held([P, P], F32, "ident")
-        nc.vector.tensor_scalar(
-            out=ident[:], in0=ramp[:], scalar1=base[:], scalar2=turned[:, 0:1], op0=ALU.subtract, op1=ALU.is_equal
-        )
+        for out, in0 in (
+            (
+                eye[:].rearrange("p (t x) -> p t x", t=PACK)[:, :, 0:L:PACK],
+                ramp[:].unsqueeze(1).to_broadcast([P, PACK, P]),
+            ),
+            (ident[:], ramp[:]),
+        ):
+            nc.vector.tensor_scalar(
+                out=out, in0=in0, scalar1=base[:], scalar2=turned[:, 0:1], op0=ALU.subtract, op1=ALU.is_equal
+            )
         nc.gpsimd.memset(sc_raw[:].bitcast(I32), 0)
-        eye_codes, eye_scales = quantize(eye[:, 0 : PACK * L], "eye")
+        nc.gpsimd.memset(wgt_rows[64:P, :], 0.0)
+        eye_q = operand("eye_q", L)
+        quantize(eye_q, 0, eye[:, 0 : PACK * L])
 
         x_planes = xT.rearrange("(a p i) t -> a i p t", a=2, i=PACK)
         c_rows = c.rearrange("(p t) j -> p t j", t=PACK)
         wt_sc32 = wt_scales.bitcast(I32).rearrange("a q n -> q a n")
         wx_sc32 = wx_scales.bitcast(I32)
         sc32 = sc_raw[:].bitcast(I32)
-
-        def load_c(h):
-            j0 = sum(C_LOADS[:h])
-            return (c_sb[h][:], c_rows[:, :, j0 : j0 + C_LOADS[h]])
-
-        small = []
+        scale_loads = []
         for Q in range(4):
-            small.append((sc32[32 * Q : 32 * Q + 4, :, :], wt_sc32[4 * Q : 4 * Q + 4, :, :]))
-            small.append((sc32[32 * Q + 4 : 32 * Q + 8, 0, :], wx_sc32[0, 4 * Q : 4 * Q + 4, :]))
-
-        def load_x(k):
-            return (x_sb[k][:], x_planes[k // PACK, k % PACK])
-
-        wgt_rows = held([P, P], F32, "wgt_rows")
-        nc.gpsimd.memset(wgt_rows[64:P, :], 0.0)
+            scale_loads.append((sc32[32 * Q : 32 * Q + 4, :, :], wt_sc32[4 * Q : 4 * Q + 4, :, :]))
+            scale_loads.append((sc32[32 * Q + 4 : 32 * Q + 8, 0, :], wx_sc32[0, 4 * Q : 4 * Q + 4, :]))
+        x_loads = [(x_sb[k][:], x_planes[k // PACK, k % PACK]) for k in range(2 * PACK)]
         wt_load = (wt_raw[:].bitcast(I32), wt_words.bitcast(I32).rearrange("a p n -> p a n"))
         wx_load = (wx_raw[:], wx_words[0].rearrange("p n i -> p (n i)").bitcast(I32))
-        bias_load = (bias[:], b.rearrange("(p t) -> p t", t=PACK))
-        loads = [(wgt_rows[0:64, :], wgt[0:P:16, :]), load_c(0), load_c(1), load_c(2), (offsets[:], offs), load_x(0)]
-        loads.extend(small[0:2] + [load_x(1)] + small[2:4] + [load_x(2)] + small[4:6] + [wt_load, load_x(3)])
-        loads.extend(small[6:8] + [wx_load, bias_load])
-        loads.extend(load_x(k) for k in range(PACK, 2 * PACK))
+        loads = [(wgt_rows[0:64, :], wgt[0:P:16, :])]
+        loads.extend((c_sb[h][:], c_rows[:, :, h * W : (h + 1) * W]) for h in range(QUARTERS))
+        loads.extend([(offsets[:], offs)] + x_loads[0:2] + scale_loads[0:2] + x_loads[2:3] + scale_loads[2:6])
+        loads.extend([wt_load, x_loads[3]] + scale_loads[6:8] + [wx_load, (bias[:], b.rearrange("(p t) -> p t", t=PACK))])
+        loads.extend(x_loads[PACK:])
         for dst, src in loads:
             nc.sync.dma_start(dst, src)
 
         turned_rows = psum.tile([P, P], F32, name="turned_rows", tag="bank")
         nc.tensor.transpose(turned_rows[:], wgt_rows[:], ident[:])
-        wgt_banks = []
+        spread = [held([P, PACK, 8, 16], F32, f"spread{u}") for u in range(2)]
         for u in range(2):
-            spread = held([P, PACK, 8, 16], F32, f"spread{u}")
             blocks = turned_rows[:, 0:64].rearrange("j (g b) -> j b g", b=8)[:, PACK * u : PACK * (u + 1), :]
-            nc.scalar.copy(out=spread[:], in_=blocks.unsqueeze(3).to_broadcast([P, PACK, 8, 16]))
-            wgt_banks.append(psum.tile([P, PACK, P], F32, name="wgt_bank", tag="bank"))
+            nc.scalar.copy(out=spread[u][:], in_=blocks.unsqueeze(3).to_broadcast([P, PACK, 8, 16]))
+        wgt_banks = {}
+
+        def turn_wgt(u):
+            wgt_banks[u] = psum.tile([P, PACK, P], F32, name="wgt_bank", tag="bank")
             for v in range(PACK):
-                nc.tensor.transpose(wgt_banks[u][:, v, :], spread[:, v, :, :].rearrange("j g r -> j (g r)"), ident[:])
+                nc.tensor.transpose(wgt_banks[u][:, v, :], spread[u][:, v, :, :].rearrange("j g r -> j (g r)"), ident[:])
 
         def take_wgt(u):
             nc.scalar.copy(out=wgt_sb[:, u * BANK : (u + 1) * BANK], in_=wgt_banks[u][:].rearrange("p v j -> p (v j)"))
 
-        def c_cols(j0, j1):
-            h = max(u for u in range(len(C_LOADS)) if sum(C_LOADS[:u]) <= j0)
-            first = sum(C_LOADS[:h])
-            return c_sb[h][:, :, j0 - first : j1 - first]
+        cb = [held([P, PACK * W], BF16, f"cb{h}") for h in range(QUARTERS)]
+        cq = [operand(f"cq{h}", W) for h in range(QUARTERS)]
+        rb_early = held([P, 2 * PACK * W], BF16, "rb_early")
+        rb = [rb_early[:, 0 : PACK * W], rb_early[:, PACK * W :]]
+        rb.extend(held([P, PACK * W], BF16, f"rb{h}")[:] for h in (2, 3))
 
-        cb = {}
-        cq = [(held([P, W], U32, f"cq{h}"), held([P, W], U8, f"cq_scales{h}")) for h in range(QUARTERS - 1)]
-        cq.append((placed([P, W], U32, "cq_last", 16), held([P, W], U8, "cq_scales_last")))
-        cr = {}
-        stage = held([P, PACK * PITCH], F32, "stage")
-        rb = [held([P, 2 * PACK * W], BF16, "rb_early")[:], stage[:, 2 * PITCH + 3 * W : 3 * PITCH].bitcast(BF16)]
-
-        def round_c(h):
-            cb[h] = held([P, PACK * W], BF16, f"cb{h}")
-            width = SUB if h <= 1 else W
+        def round_c(h, pieces, on_vector):
+            width = W // pieces
             for j0 in range(0, W, width):
-                weave(cb[h][:, PACK * j0 : PACK * (j0 + width)], c_cols(h * W + j0, h * W + j0 + width), h == 0)
+                weave(woven(cb[h][:, PACK * j0 : PACK * (j0 + width)]), c_sb[h][:, :, j0 : j0 + width], on_vector)
 
-        def first_tier(h):
-            width = SUB if h <= 1 else W
+        def first_tier(h, pieces):
+            width = W // pieces
             for j0 in range(0, W, width):
-                quantize_into(cq[h], j0, cb[h][:, PACK * j0 : PACK * (j0 + width)])
+                quantize(cq[h], j0, cb[h][:, PACK * j0 : PACK * (j0 + width)])
 
-        def leftover(h):
-            codes, scales = cq[h]
-            backs = []
+        def decode(h, s):
+            cols = slice(s * SUB, (s + 1) * SUB)
+            back = psum.tile([P, PACK, SUB], F32, name="back", tag="bank")
+            for t in range(PACK):
+                nc.tensor.matmul_mx(
+                    out=back[:, t, :],
+                    lhsT=eye_q[0][:, t * P : (t + 1) * P].bitcast(FP8X4),
+                    lhsT_scale=eye_q[1][:, t * P : (t + 1) * P],
+                    rhs=cq[h][0][:, cols].bitcast(FP8X4),
+                    rhs_scale=cq[h][1][:, cols],
+                    start=True,
+                    stop=True,
+                )
+            return back
+
+        def leftover_on_vector(h):
             for s in range(W // SUB):
-                cols = slice(s * SUB, (s + 1) * SUB)
-                at = (h % 2 * W + s * SUB) * PACK
-                back = psum.tile([P, PACK, SUB], F32, name="back", tag="bank")
-                for t in range(PACK):
-                    nc.tensor.matmul_mx(
-                        out=back[:, t, :],
-                        lhsT=eye_codes[:, t * P : (t + 1) * P].bitcast(FP8X4),
-                        lhsT_scale=eye_scales[:, t * P : (t + 1) * P],
-                        rhs=codes[:, cols].bitcast(FP8X4),
-                        rhs_scale=scales[:, cols],
-                        start=True,
-                        stop=True,
-                    )
-                if h in IN_PSUM:
-                    backs.append(back)
-                else:
-                    nc.vector.tensor_tensor(
-                        out=woven(rb[h // 2][:, at : at + PACK * SUB]),
-                        in0=planar(c_cols(h * W + s * SUB, h * W + (s + 1) * SUB)),
-                        in1=planar(back[:]),
-                        op=ALU.subtract,
-                    )
-            if h in IN_PSUM:
-                turn_c(h)
-                leftover_in_psum(h, backs)
+                back = decode(h, s)
+                nc.vector.tensor_tensor(
+                    out=woven(rb[h][:, s * PACK * SUB : (s + 1) * PACK * SUB]),
+                    in0=planar(c_sb[h][:, :, s * SUB : (s + 1) * SUB]),
+                    in1=planar(back[:]),
+                    op=ALU.subtract,
+                )
 
-        rests = {}
+        def add_turned(rest, src, first):
+            for t in range(PACK):
+                nc.tensor.matmul(
+                    rest[:, t, :],
+                    lhsT=src[:, t, :],
+                    rhs=ident[:],
+                    is_transpose=True,
+                    start=first and t == 0,
+                    stop=not first and t == PACK - 1,
+                )
 
-        def turn_c(h):
-            for s in range(W // SUB):
-                rests[h, s] = psum.tile([P, PACK, P], F32, name="rest", tag="bank")
-                src = c_cols(h * W + s * SUB, h * W + (s + 1) * SUB)
-                for t in range(PACK):
-                    nc.tensor.matmul(
-                        rests[h, s][:, t, :], lhsT=src[:, t, :], rhs=ident[:], is_transpose=True, start=t == 0, stop=False
-                    )
-
-        def leftover_in_psum(h, backs):
+        def leftover_in_psum(h):
+            pieces = range(W // SUB)
+            backs = [decode(h, s) for s in pieces]
+            rests = []
+            for s in pieces:
+                rests.append(psum.tile([P, PACK, P], F32, name="rest", tag="bank"))
+                add_turned(rests[s], c_sb[h][:, :, s * SUB : (s + 1) * SUB], True)
             minus = []
-            for s, back in enumerate(backs):
+            for s in pieces:
                 if (h, s) == (QUARTERS - 1, 0):
-                    minus.append(placed([P, PACK, SUB], F32, "minus_last", 24))
+                    minus.append(placed([P, PACK, SUB], F32, "minus_last", 32))
                 else:
                     minus.append(held([P, PACK, SUB], F32, f"minus{h}_{s}"))
-                nc.scalar.activation(out=minus[s][:], in_=back[:], func=ACT.Identity, scale=-1.0)
+                nc.scalar.activation(out=minus[s][:], in_=backs[s][:], func=ACT.Identity, scale=-1.0)
             pairs = []
-            for s in range(W // SUB):
-                rest = rests[h, s]
-                for t in range(PACK):
-                    nc.tensor.matmul(
-                        rest[:, t, :],
-                        lhsT=minus[s][:, t, :],
-                        rhs=ident[:],
-                        is_transpose=True,
-                        start=False,
-                        stop=t == PACK - 1,
-                    )
+            for s in pieces:
+                add_turned(rests[s], minus[s], False)
                 pairs.append(held([P, 2, P, 2], BF16, f"pairs{h}_{s}"))
                 nc.scalar.activation(
-                    out=pairs[s][:], in_=rest[:].rearrange("j (u e) p -> j u p e", e=2), func=ACT.Identity
+                    out=pairs[s][:], in_=rests[s][:].rearrange("j (u e) p -> j u p e", e=2), func=ACT.Identity
                 )
             words = psum.tile([P, W // SUB, 2, SUB], F32, name="words", tag="bank")
-            for s in range(W // SUB):
+            for s in pieces:
                 as_words = pairs[s][:].rearrange("j u p e -> j (u p e)").bitcast(F32)
                 for u in range(2):
                     nc.tensor.transpose(words[:, s, u, :], as_words[:, u * P : (u + 1) * P], ident[:])
-            at = h % 2 * W * PACK
             nc.scalar.copy(
-                out=rb[h // 2][:, at : at + PACK * W].bitcast(F32).rearrange("p (s j u) -> p s j u", s=W // SUB, u=2),
+                out=rb[h].bitcast(F32).rearrange("p (s j u) -> p s j u", s=W // SUB, u=2),
                 in_=words[:].rearrange("p s u j -> p s j u"),
             )
-
-        def second_tier(h):
-            codes = placed([P, 2 * W], U32, "cr_late", 2) if h else held([P, 2 * W], U32, "cr_early")
-            cr[h] = (codes, held([P, 2 * W], U8, f"cr_scales{h}"))
-            quantize_into(cr[h], 0, rb[h])
 
         def gather(dst, k, j0, j1):
             nc.vector.tensor_tensor(
@@ -260,24 +226,27 @@ def tile_list_biasP_kernel(
                 op=ALU.mult,
             )
 
-        round_c(0)
-        round_c(1)
+        turn_wgt(0)
+        round_c(0, 2, True)
+        round_c(1, 2, False)
+        first_tier(0, 2)
+        first_tier(1, 2)
+        leftover_on_vector(0)
+        leftover_on_vector(1)
+        turn_wgt(1)
+        round_c(2, 1, False)
         take_wgt(0)
+        round_c(3, 1, False)
         take_wgt(1)
+        first_tier(2, 1)
+        first_tier(3, 1)
+        cr_early = operand("cr_early", 2 * W)
+        quantize(cr_early, 0, rb_early[:])
         picked0 = held([P, PACK, J], F32, "picked0")
-        for h in range(QUARTERS + 2):
-            if h == 2:
-                leftover(1)
-                round_c(2)
-                round_c(3)
-            if h == QUARTERS - 1:
-                gather(picked0[:, 0, :], 0, 0, J)
-            if h < QUARTERS:
-                first_tier(h)
-            if 1 <= h <= QUARTERS and h != 2:
-                leftover(h - 1)
-            if h == 3:
-                second_tier(0)
+        gather(picked0[:, 0, 0:BANK], 0, 0, BANK)
+        gather(picked0[:, 0, BANK:J], 0, BANK, J)
+        leftover_in_psum(2)
+        leftover_in_psum(3)
 
         wt_d = held([P, 2 * 2 * N], U8, "wt_d")
         nc.scalar.copy(
@@ -301,177 +270,143 @@ def tile_list_biasP_kernel(
             per_bank = BANK // WIDTHS[n]
             return banks[n, t // per_bank][:, t % per_bank, :]
 
-        def wx_pass(n, t, operand, cols, start):
-            codes, scales = operand
-            nc.tensor.matmul_mx(
-                out=sum_of(n, t),
-                lhsT=wx_d[:, t * P : (t + 1) * P].bitcast(FP8X4),
-                lhsT_scale=sc_d[4:P, t * P : (t + 1) * P],
-                rhs=codes[:, cols].bitcast(FP8X4),
-                rhs_scale=scales[:, cols],
-                start=start,
-                stop=False,
-            )
+        def passes(n, weights, moving, first, opens=False, closes=False):
+            cols = slice(STARTS[n] - first, STARTS[n] - first + WIDTHS[n])
+            per_bank = BANK // WIDTHS[n]
+            for t in range(PACK):
+                if weights == "wx":
+                    lhsT = wx_d[:, t * P : (t + 1) * P].bitcast(FP8X4)
+                    lhsT_scale = sc_d[4:P, t * P : (t + 1) * P]
+                else:
+                    at = weights * N + t * P
+                    lhsT = wt_d[:, 2 * at : 2 * (at + P)].bitcast(FP4X4)
+                    lhsT_scale = sc_d[:, at : at + P]
+                nc.tensor.matmul_mx(
+                    out=sum_of(n, t),
+                    lhsT=lhsT,
+                    lhsT_scale=lhsT_scale,
+                    rhs=moving[0][:, cols].bitcast(FP8X4),
+                    rhs_scale=moving[1][:, cols],
+                    start=opens and t % per_bank == 0,
+                    stop=closes and t % per_bank == per_bank - 1,
+                )
 
-        def wt_pass(n, t, a, operand, last):
-            codes, scales, first = operand[STARTS[n]]
-            cols = slice(first, first + WIDTHS[n])
-            nc.tensor.matmul_mx(
-                out=sum_of(n, t),
-                lhsT=wt_d[:, (a * N + t * P) * 2 : (a * N + (t + 1) * P) * 2].bitcast(FP4X4),
-                lhsT_scale=sc_d[:, a * N + t * P : a * N + (t + 1) * P],
-                rhs=codes[:, cols].bitcast(FP8X4),
-                rhs_scale=scales[:, cols],
-                start=False,
-                stop=last,
-            )
+        def chunks_of(h):
+            return [n for n in range(len(WIDTHS)) if STARTS[n] // W == h]
 
-        def open_sums(n):
-            h, first = divmod(STARTS[n], W)
-            cols = slice(first, first + WIDTHS[n])
+        for n in range(len(WIDTHS)):
+            h = STARTS[n] // W
             per_bank = BANK // WIDTHS[n]
             for u in range(PACK // per_bank):
                 banks[n, u] = psum.tile([P, per_bank, WIDTHS[n]], F32, name="acc", tag="bank")
-            for t in range(PACK):
-                wx_pass(n, t, cq[h], cols, t % per_bank == 0)
-
-        def add_second_tier(n):
-            half, first = divmod(STARTS[n], 2 * W)
-            for t in range(PACK):
-                wx_pass(n, t, cr[half], slice(first, first + WIDTHS[n]), False)
-
-        for n in range(len(WIDTHS)):
-            open_sums(n)
-            if STARTS[n] < 2 * W:
-                add_second_tier(n)
+            passes(n, "wx", cq[h], h * W, opens=True)
+            if h < 2:
+                passes(n, "wx", cr_early, 0)
 
         for k in range(1, PACK):
             gather(picked0[:, k, :], k, 0, J)
-        xb0 = [placed([P, 2 * PACK * W], BF16, f"xb0_{u}", 24 + 4 * u)[:] for u in range(2)]
+        xb0_early = placed([P, 2 * PACK * W], BF16, "xb0_early", 32)
         for t0 in (0, 2):
-            nc.scalar.activation(
-                out=woven(xb0[0])[:, :, t0 : t0 + 2, :],
-                in_=planar(picked0[:, t0 : t0 + 2, 0 : 2 * W]),
-                func=ACT.Identity,
-            )
-        weave(xb0[1], picked0[:, :, 2 * W : J], False)
-
-        xq0 = {}
-
-        def first_pass(u):
-            codes = placed([P, 2 * W], U32, f"xq0_codes{u}", 10 if u else 0)
-            scales = held([P, 2 * W], U8, f"xq0_scales{u}")
-            quantize_into((codes, scales), 0, xb0[u])
-            for j0 in range(u * 2 * W, (u + 1) * 2 * W, SUB):
-                xq0[j0] = (codes, scales, j0 - u * 2 * W)
-
-        def add_first_pass(u):
-            for n in range(len(WIDTHS)):
-                if STARTS[n] // (2 * W) == u:
-                    for t in range(PACK):
-                        wt_pass(n, t, 0, xq0, False)
+            weave(woven(xb0_early[:])[:, :, t0 : t0 + 2, :], picked0[:, t0 : t0 + 2, 0 : 2 * W], False)
+        xb0 = {h: held([P, PACK * W], BF16, f"xb0_{h}") for h in (2, 3)}
 
         out_rows = out_0.rearrange("(p t) j -> p t j", t=PACK)
         out_words = out_1[0].rearrange("p j i -> p (j i)").bitcast(I32)
         y_scales = held([P, J], U8, "y_scales")
-        picked1 = stage[:].rearrange("p (t j) -> p t j", t=PACK)
-        xb1 = {0: picked1[:, 3, 3 * W : J + W].bitcast(BF16), 1: picked1[:, 1, 2 * W : J].bitcast(BF16)}
-        xb1_late = held([P, PACK * 2 * W], BF16, "xb1_late")
-        for n in range(2, len(WIDTHS)):
-            first = PACK * (STARTS[n] - 2 * W)
-            xb1[n] = xb1_late[:, first : first + PACK * WIDTHS[n]]
         y = [held([P, PACK, W], F32, f"y{h}") for h in range(QUARTERS)]
         yb = [held([P, PACK * W], BF16, f"yb{h}") for h in range(QUARTERS)]
 
-        def pick(i, j0, j1):
-            gather(picked1[:, i, j0:j1], PACK + i, j0, j1)
+        stage = held([P, 20 * W], F32, "stage")
 
-        def round_pair(dst, t0, j0, on_vector):
-            out = woven(dst)[:, :, t0 : t0 + 2, :]
-            src = planar(picked1[:, t0 : t0 + 2, j0 : j0 + dst.shape[1] // PACK])
-            if on_vector:
-                nc.vector.tensor_copy(out=out, in_=src)
-            else:
-                nc.scalar.activation(out=out, in_=src, func=ACT.Identity)
+        def rows(first, pitch, count, width):
+            return stage[:, first * W : (first + count * pitch) * W].rearrange("p (t j) -> p t j", t=count)[:, :, 0:width]
+
+        low_early = rows(0, 10, 2, 2 * W)
+        low_third = rows(2, 3, 2, W)
+        high = rows(12, 3, 2, 3 * W)
+        last = rows(3, 2, PACK, W)
+        xb1 = {
+            0: stage[:, 4 * W : 6 * W].bitcast(BF16),
+            1: placed([P, PACK * W], BF16, "xb1_1", 36)[:],
+            2: stage[:, 7 * W + SUB : 9 * W + SUB].bitcast(BF16),
+            3: held([P, PACK * W], BF16, "xb1_3")[:],
+        }
+
+        def round_pair(h, t0, src, on_vector):
+            weave(woven(xb1[h])[:, :, t0 : t0 + 2, :], src, on_vector)
+
+        def add_quarter(h, weights, name, src, kib):
+            codes = operand(name, W, kib)
+            quantize(codes, 0, src)
+            for n in chunks_of(h):
+                passes(n, weights, codes, h * W)
 
         def close_sums(n):
-            per_bank = BANK // WIDTHS[n]
-            codes, scales = quantize(xb1[n], f"xq1_{n}")
-            xq1 = {STARTS[n] + j: (codes, scales, j) for j in range(0, WIDTHS[n], SUB)}
-            for t in range(PACK):
-                wt_pass(n, t, 1, xq1, t % per_bank == per_bank - 1)
+            h, first = divmod(STARTS[n], W)
+            codes = operand(f"xq1_{n}", WIDTHS[n])
+            quantize(codes, 0, xb1[h][:, PACK * first : PACK * (first + WIDTHS[n])])
+            passes(n, 1, codes, STARTS[n], closes=True)
 
         def add_bias(h):
-            chunks = [n for n in range(len(WIDTHS)) if STARTS[n] // W == h]
-            for t0 in (0, 2):
-                for n in chunks:
-                    first = STARTS[n] - h * W
-                    for t in (t0, t0 + 1):
-                        dst = y[h][:, t, first : first + WIDTHS[n]]
-                        nc.scalar.activation(out=dst, in_=sum_of(n, t), func=ACT.Identity, bias=bias[:, t : t + 1])
-                nc.sync.dma_start(out_rows[:, t0 : t0 + 2, h * W : (h + 1) * W], y[h][:, t0 : t0 + 2, :])
+            for n in chunks_of(h):
+                first = STARTS[n] - h * W
+                for t in range(PACK):
+                    dst = y[h][:, t, first : first + WIDTHS[n]]
+                    nc.scalar.activation(out=dst, in_=sum_of(n, t), func=ACT.Identity, bias=bias[:, t : t + 1])
+                    if n == chunks_of(h)[-1] and t % 2 == 1:
+                        pair = slice(t - 1, t + 1)
+                        nc.sync.dma_start(out_rows[:, pair, h * W : (h + 1) * W], y[h][:, pair, :])
 
-        def round_y(n):
+        def round_y(n, on_vector):
             h, first = divmod(STARTS[n], W)
-            dst = yb[h][:, PACK * first : PACK * (first + WIDTHS[n])]
-            weave(dst, y[h][:, :, first : first + WIDTHS[n]], n not in Y_ROUND_ON_SCALAR)
+            cols = slice(first, first + WIDTHS[n])
+            weave(woven(yb[h][:, PACK * cols.start : PACK * cols.stop]), y[h][:, :, cols], on_vector)
 
-        def round_sums(n):
-            h, first = divmod(STARTS[n], W)
-            dst = yb[h][:, PACK * first : PACK * (first + WIDTHS[n])]
-            nc.vector.tensor_tensor(
-                out=dst.rearrange("p (j t) -> p j t", t=PACK),
-                in0=banks[n, 0][:].rearrange("p t j -> p j t"),
-                in1=bias[:].unsqueeze(1).to_broadcast([P, WIDTHS[n], PACK]),
-                op=ALU.add,
-            )
-
-        def hand_on(n):
-            cols = slice(n * W, (n + 1) * W)
-            y_codes = held([P, W], U32, f"y_codes{n}")
-            nc.vector.quantize_mx(out=y_codes[:].bitcast(FP8X4), scales=y_scales[:, cols], in_=yb[n][:])
+        def hand_on(h):
+            cols = slice(h * W, (h + 1) * W)
+            y_codes = held([P, W], U32, f"y_codes{h}")
+            nc.vector.quantize_mx(out=y_codes[:].bitcast(FP8X4), scales=y_scales[:, cols], in_=yb[h][:])
             nc.sync.dma_start(out_words[:, cols], y_codes[:].bitcast(I32))
 
-        pick(0, 0, J)
-        pick(1, 0, 2 * W)
-        round_pair(xb1[0], 0, 0, False)
-        round_pair(xb1[1], 0, W, False)
-        first_pass(0)
-        add_first_pass(0)
-        second_tier(1)
-        pick(2, 0, J)
-        for n in range(2, len(WIDTHS)):
-            add_second_tier(n)
-        pick(3, 0, W)
-        pick(3, W, 2 * W)
-        pick(3, 2 * W, 3 * W)
+        for h in (2, 3):
+            weave(woven(xb0[h][:]), picked0[:, :, h * W : (h + 1) * W], False)
+        gather(stage[:, 0:J], PACK, 0, J)
+        gather(low_early[:, 1, :], PACK + 1, 0, 2 * W)
+        for h in (0, 1):
+            round_pair(h, 0, low_early[:, :, h * W : (h + 1) * W], False)
+        xq0_early = operand("xq0_early", 2 * W, 0)
+        quantize(xq0_early, 0, xb0_early[:])
+        for n in (0, 1):
+            passes(n, 0, xq0_early, 0)
+        gather(high[:, 0, :], PACK + 2, 0, 3 * W)
         for h in range(3):
-            round_pair(xb1[h], 2, h * W, False)
+            gather(high[:, 1, h * W : (h + 1) * W], PACK + 3, h * W, (h + 1) * W)
+        for h in range(3):
+            round_pair(h, 2, high[:, :, h * W : (h + 1) * W], False)
         close_sums(0)
-        pick(3, 3 * W, J)
+        gather(low_third[:, 1, :], PACK + 1, 2 * W, 3 * W)
         close_sums(1)
-        first_pass(1)
-        add_first_pass(1)
-        add_bias(0)
-        add_bias(1)
-        round_y(0)
-        weave(yb[1][:, 0 : PACK * SUB], y[1][:, :, 0:SUB], False)
-        pick(1, 2 * W, 3 * W)
-        round_pair(xb1[2], 0, STARTS[2], True)
-        pick(1, 3 * W, J)
+        round_pair(2, 0, low_third, True)
+        add_quarter(2, 0, "xq0_2", xb0[2][:], 36)
+        add_quarter(2, "wx", "cr_2", rb[2], 37)
         close_sums(2)
-        weave(xb1_late[:, PACK * W :], picked1[:, :, 3 * W : J], True)
+        for h in range(3):
+            add_bias(h)
+        for i in range(1, PACK):
+            gather(last[:, i, :], PACK + i, 3 * W, J)
+        add_quarter(3, 0, "xq0_3", xb0[3][:], 8)
+        weave(woven(xb1[3]), last, True)
+        add_quarter(3, "wx", "cr_3", rb[3], 16)
         close_sums(3)
         close_sums(4)
-        round_sums(4)
-        add_bias(2)
+        round_y(0, False)
+        round_y(1, False)
         add_bias(3)
-        hand_on(0)
-        weave(yb[1][:, PACK * SUB :], y[1][:, :, SUB:W], True)
-        hand_on(1)
-        round_y(2)
-        round_y(3)
-        hand_on(2)
+        round_y(2, True)
+        for h in (2, 0, 1):
+            hand_on(h)
+        round_y(3, True)
+        round_y(4, True)
         hand_on(3)
         for Q in range(4):
             (nc.sync if Q % 2 == 0 else nc.scalar).dma_start(

@@ -68,9 +68,10 @@ def tile_list_biasP_kernel(
         bias = held([P, PACK], F32, "bias")
         wgt_sb = held([P, J], F32, "wgt_sb")
         wgt_rows = held([P, P], F32, "wgt_rows")
-        x_sb = [held([P, T], F32, f"x{k}") for k in range(PACK)]
+        x_sb = [placed([P, T], F32, "x0", 40)] + [held([P, T], F32, f"x{k}") for k in range(1, PACK)]
         x_sb.extend(placed([P, T], F32, f"x{PACK + i}", 8 * i) for i in range(PACK))
-        c_sb = [held([P, PACK, W], F32, f"c{h}") for h in range(QUARTERS)]
+        c_late = held([P, PACK, 2 * W], F32, "c_late")
+        c_sb = [held([P, PACK, W], F32, f"c{h}")[:] for h in range(2)] + [c_late[:, :, 0:W], c_late[:, :, W:]]
 
         eye = held([P, PACK * (L + 1)], BF16, "eye")
         ones = held([P, P], F32, "ones")
@@ -112,8 +113,9 @@ def tile_list_biasP_kernel(
         wt_load = (wt_raw[:].bitcast(I32), wt_words.bitcast(I32).rearrange("a p n -> p a n"))
         wx_load = (wx_raw[:], wx_words[0].rearrange("p n i -> p (n i)").bitcast(I32))
         loads = [(wgt_rows[0:64, :], wgt[0:P:16, :])]
-        loads.extend((c_sb[h][:], c_rows[:, :, h * W : (h + 1) * W]) for h in range(QUARTERS))
-        loads.extend([(offsets[:], offs)] + x_loads[0:2] + scale_loads[0:2] + x_loads[2:3] + scale_loads[2:6])
+        loads.extend((c_sb[h], c_rows[:, :, h * W : (h + 1) * W]) for h in range(2))
+        loads.extend([(c_late[:], c_rows[:, :, 2 * W :]), (offsets[:], offs), x_loads[0]] + scale_loads[0:2])
+        loads.extend([x_loads[1]] + scale_loads[2:4] + [x_loads[2]] + scale_loads[4:6])
         loads.extend([wt_load, x_loads[3]] + scale_loads[6:8] + [wx_load, (bias[:], b.rearrange("(p t) -> p t", t=PACK))])
         loads.extend(x_loads[PACK:])
         for dst, src in loads:
@@ -136,10 +138,11 @@ def tile_list_biasP_kernel(
             nc.scalar.copy(out=wgt_sb[:, u * BANK : (u + 1) * BANK], in_=wgt_banks[u][:].rearrange("p v j -> p (v j)"))
 
         cb = [held([P, PACK * W], BF16, f"cb{h}") for h in range(QUARTERS)]
-        cq = [operand(f"cq{h}", W) for h in range(QUARTERS)]
+        cq = [operand(f"cq{h}", W) for h in range(QUARTERS - 1)] + [operand("cq_last", W, 40)]
         rb_early = held([P, 2 * PACK * W], BF16, "rb_early")
         rb = [rb_early[:, 0 : PACK * W], rb_early[:, PACK * W :]]
-        rb.extend(held([P, PACK * W], BF16, f"rb{h}")[:] for h in (2, 3))
+        rb_late = held([P, 2 * PACK * W], BF16, "rb_late")
+        rb.extend([rb_late[:, 0 : PACK * W], rb_late[:, PACK * W :]])
 
         def round_c(h, pieces, on_vector):
             width = W // pieces
@@ -227,25 +230,24 @@ def tile_list_biasP_kernel(
             )
 
         turn_wgt(0)
+        turn_wgt(1)
         round_c(0, 2, True)
         round_c(1, 2, False)
+        take_wgt(0)
+        take_wgt(1)
         first_tier(0, 2)
         first_tier(1, 2)
         leftover_on_vector(0)
         leftover_on_vector(1)
-        turn_wgt(1)
         round_c(2, 1, False)
-        take_wgt(0)
         round_c(3, 1, False)
-        take_wgt(1)
         first_tier(2, 1)
+        picked0 = held([P, PACK, J], F32, "picked0")
+        gather(picked0[:, 0, :], 0, 0, J)
         first_tier(3, 1)
+        leftover_in_psum(2)
         cr_early = operand("cr_early", 2 * W)
         quantize(cr_early, 0, rb_early[:])
-        picked0 = held([P, PACK, J], F32, "picked0")
-        gather(picked0[:, 0, 0:BANK], 0, 0, BANK)
-        gather(picked0[:, 0, BANK:J], 0, BANK, J)
-        leftover_in_psum(2)
         leftover_in_psum(3)
 
         wt_d = held([P, 2 * 2 * N], U8, "wt_d")
@@ -308,7 +310,7 @@ def tile_list_biasP_kernel(
         xb0_early = placed([P, 2 * PACK * W], BF16, "xb0_early", 32)
         for t0 in (0, 2):
             weave(woven(xb0_early[:])[:, :, t0 : t0 + 2, :], picked0[:, t0 : t0 + 2, 0 : 2 * W], False)
-        xb0 = {h: held([P, PACK * W], BF16, f"xb0_{h}") for h in (2, 3)}
+        xb0_late = held([P, 2 * PACK * W], BF16, "xb0_late")
 
         out_rows = out_0.rearrange("(p t) j -> p t j", t=PACK)
         out_words = out_1[0].rearrange("p j i -> p (j i)").bitcast(I32)
@@ -327,19 +329,13 @@ def tile_list_biasP_kernel(
         last = rows(3, 2, PACK, W)
         xb1 = {
             0: stage[:, 4 * W : 6 * W].bitcast(BF16),
-            1: placed([P, PACK * W], BF16, "xb1_1", 36)[:],
+            1: placed([P, PACK * W], BF16, "xb1_1", 37)[:],
             2: stage[:, 7 * W + SUB : 9 * W + SUB].bitcast(BF16),
             3: held([P, PACK * W], BF16, "xb1_3")[:],
         }
 
         def round_pair(h, t0, src, on_vector):
             weave(woven(xb1[h])[:, :, t0 : t0 + 2, :], src, on_vector)
-
-        def add_quarter(h, weights, name, src, kib):
-            codes = operand(name, W, kib)
-            quantize(codes, 0, src)
-            for n in chunks_of(h):
-                passes(n, weights, codes, h * W)
 
         def close_sums(n):
             h, first = divmod(STARTS[n], W)
@@ -368,8 +364,7 @@ def tile_list_biasP_kernel(
             nc.vector.quantize_mx(out=y_codes[:].bitcast(FP8X4), scales=y_scales[:, cols], in_=yb[h][:])
             nc.sync.dma_start(out_words[:, cols], y_codes[:].bitcast(I32))
 
-        for h in (2, 3):
-            weave(woven(xb0[h][:]), picked0[:, :, h * W : (h + 1) * W], False)
+        weave(woven(xb0_late[:]), picked0[:, :, 2 * W :], False)
         gather(stage[:, 0:J], PACK, 0, J)
         gather(low_early[:, 1, :], PACK + 1, 0, 2 * W)
         for h in (0, 1):
@@ -387,23 +382,29 @@ def tile_list_biasP_kernel(
         gather(low_third[:, 1, :], PACK + 1, 2 * W, 3 * W)
         close_sums(1)
         round_pair(2, 0, low_third, True)
-        add_quarter(2, 0, "xq0_2", xb0[2][:], 36)
-        add_quarter(2, "wx", "cr_2", rb[2], 37)
+        xq0_late = operand("xq0_late", 2 * W, 36)
+        quantize(xq0_late, 0, xb0_late[:])
+        passes(2, 0, xq0_late, 2 * W)
+        cr_late = operand("cr_late", 2 * W, 38)
+        quantize(cr_late, 0, rb_late[:])
+        passes(2, "wx", cr_late, 2 * W)
         close_sums(2)
-        for h in range(3):
-            add_bias(h)
+        for n in (3, 4):
+            passes(n, 0, xq0_late, 2 * W)
+            passes(n, "wx", cr_late, 2 * W)
+        add_bias(0)
+        add_bias(1)
+        round_y(0, False)
+        add_bias(2)
         for i in range(1, PACK):
             gather(last[:, i, :], PACK + i, 3 * W, J)
-        add_quarter(3, 0, "xq0_3", xb0[3][:], 8)
         weave(woven(xb1[3]), last, True)
-        add_quarter(3, "wx", "cr_3", rb[3], 16)
         close_sums(3)
         close_sums(4)
-        round_y(0, False)
         round_y(1, False)
         add_bias(3)
         round_y(2, True)
-        for h in (2, 0, 1):
+        for h in (0, 2, 1):
             hand_on(h)
         round_y(3, True)
         round_y(4, True)

@@ -68,7 +68,7 @@ def tile_list_biasP_kernel(
         bias = held([P, PACK], F32, "bias")
         wgt_sb = held([P, J], F32, "wgt_sb")
         wgt_rows = held([P, P], F32, "wgt_rows")
-        x_sb = [placed([P, T], F32, "x0", 40)] + [held([P, T], F32, f"x{k}") for k in range(1, PACK)]
+        x_sb = [placed([P, T], F32, "x0", 40)] + [held([P, T], F32, f"x{k}") for k in (1, 2)] + [placed([P, T], F32, "x3", 48)]
         x_sb.extend(placed([P, T], F32, f"x{PACK + i}", 8 * i) for i in range(PACK))
         c_late = held([P, PACK, 2 * W], F32, "c_late")
         c_sb = [held([P, PACK, W], F32, f"c{h}")[:] for h in range(2)] + [c_late[:, :, 0:W], c_late[:, :, W:]]
@@ -116,8 +116,8 @@ def tile_list_biasP_kernel(
         loads.extend((c_sb[h], c_rows[:, :, h * W : (h + 1) * W]) for h in range(2))
         loads.extend([(c_late[:], c_rows[:, :, 2 * W :]), (offsets[:], offs), x_loads[0]] + scale_loads[0:2])
         loads.extend([x_loads[1]] + scale_loads[2:4] + [x_loads[2]] + scale_loads[4:6])
-        loads.extend([wt_load, x_loads[3]] + scale_loads[6:8] + [wx_load, (bias[:], b.rearrange("(p t) -> p t", t=PACK))])
-        loads.extend(x_loads[PACK:])
+        loads.extend([wt_load, x_loads[3]] + scale_loads[6:8] + [wx_load])
+        loads.extend(x_loads[PACK:] + [(bias[:], b.rearrange("(p t) -> p t", t=PACK))])
         for dst, src in loads:
             nc.sync.dma_start(dst, src)
 
@@ -141,8 +141,7 @@ def tile_list_biasP_kernel(
         cq = [operand(f"cq{h}", W) for h in range(QUARTERS - 1)] + [operand("cq_last", W, 40)]
         rb_early = held([P, 2 * PACK * W], BF16, "rb_early")
         rb = [rb_early[:, 0 : PACK * W], rb_early[:, PACK * W :]]
-        rb_late = held([P, 2 * PACK * W], BF16, "rb_late")
-        rb.extend([rb_late[:, 0 : PACK * W], rb_late[:, PACK * W :]])
+        rb.extend(held([P, PACK * W], BF16, f"rb{h}")[:] for h in (2, 3))
 
         def round_c(h, pieces, on_vector):
             width = W // pieces
@@ -365,6 +364,9 @@ def tile_list_biasP_kernel(
             nc.sync.dma_start(out_words[:, cols], y_codes[:].bitcast(I32))
 
         weave(woven(xb0_late[:]), picked0[:, :, 2 * W :], False)
+        cr_third = operand("cr_third", W, 48)
+        quantize(cr_third, 0, rb[2])
+        passes(2, "wx", cr_third, 2 * W)
         gather(stage[:, 0:J], PACK, 0, J)
         gather(low_early[:, 1, :], PACK + 1, 0, 2 * W)
         for h in (0, 1):
@@ -385,13 +387,12 @@ def tile_list_biasP_kernel(
         xq0_late = operand("xq0_late", 2 * W, 36)
         quantize(xq0_late, 0, xb0_late[:])
         passes(2, 0, xq0_late, 2 * W)
-        cr_late = operand("cr_late", 2 * W, 38)
-        quantize(cr_late, 0, rb_late[:])
-        passes(2, "wx", cr_late, 2 * W)
         close_sums(2)
+        cr_last = operand("cr_last", W, 38)
+        quantize(cr_last, 0, rb[3])
         for n in (3, 4):
             passes(n, 0, xq0_late, 2 * W)
-            passes(n, "wx", cr_late, 2 * W)
+            passes(n, "wx", cr_last, 3 * W)
         add_bias(0)
         add_bias(1)
         round_y(0, False)

@@ -68,7 +68,7 @@ def tile_list_biasP_kernel(
         bias = held([P, PACK], F32, "bias")
         wgt_sb = held([P, J], F32, "wgt_sb")
         wgt_rows = held([P, P], F32, "wgt_rows")
-        x_sb = [placed([P, T], F32, "x0", 40)] + [held([P, T], F32, f"x{k}") for k in (1, 2)] + [placed([P, T], F32, "x3", 48)]
+        x_sb = [held([P, T], F32, f"x{k}") for k in range(3)] + [placed([P, T], F32, "x3", 48)]
         x_sb.extend(placed([P, T], F32, f"x{PACK + i}", 8 * i) for i in range(PACK))
         c_late = held([P, PACK, 2 * W], F32, "c_late")
         c_sb = [held([P, PACK, W], F32, f"c{h}")[:] for h in range(2)] + [c_late[:, :, 0:W], c_late[:, :, W:]]
@@ -138,7 +138,7 @@ def tile_list_biasP_kernel(
             nc.scalar.copy(out=wgt_sb[:, u * BANK : (u + 1) * BANK], in_=wgt_banks[u][:].rearrange("p v j -> p (v j)"))
 
         cb = [held([P, PACK * W], BF16, f"cb{h}") for h in range(QUARTERS)]
-        cq = [operand(f"cq{h}", W) for h in range(QUARTERS - 1)] + [operand("cq_last", W, 40)]
+        cq = [operand(f"cq{h}", W) for h in range(QUARTERS)]
         rb_early = held([P, 2 * PACK * W], BF16, "rb_early")
         rb = [rb_early[:, 0 : PACK * W], rb_early[:, PACK * W :]]
         rb.extend(held([P, PACK * W], BF16, f"rb{h}")[:] for h in (2, 3))
@@ -242,11 +242,11 @@ def tile_list_biasP_kernel(
         round_c(3, 1, False)
         first_tier(2, 1)
         picked0 = held([P, PACK, J], F32, "picked0")
-        gather(picked0[:, 0, :], 0, 0, J)
-        first_tier(3, 1)
-        leftover_in_psum(2)
         cr_early = operand("cr_early", 2 * W)
         quantize(cr_early, 0, rb_early[:])
+        first_tier(3, 1)
+        gather(picked0[:, 0, :], 0, 0, J)
+        leftover_in_psum(2)
         leftover_in_psum(3)
 
         wt_d = held([P, 2 * 2 * N], U8, "wt_d")

@@ -63,7 +63,7 @@ def tile_list_biasP_kernel(
 
         offsets = held([P, J // 16], U16, "offsets")
         wt_raw = held([P, 2, 2 * N], U8, "wt_raw")
-        wx_raw = held([P, N], I32, "wx_raw")
+        wx_raw = placed([P, N], I32, "wx_raw", 40)
         sc_raw = held([P, 2, N], U8, "sc_raw")
         bias = held([P, PACK], F32, "bias")
         wgt_sb = held([P, J], F32, "wgt_sb")
@@ -116,8 +116,8 @@ def tile_list_biasP_kernel(
         loads.extend((c_sb[h], c_rows[:, :, h * W : (h + 1) * W]) for h in range(2))
         loads.extend([(c_late[:], c_rows[:, :, 2 * W :]), (offsets[:], offs), x_loads[0]] + scale_loads[0:2])
         loads.extend([x_loads[1]] + scale_loads[2:4] + [x_loads[2]] + scale_loads[4:6])
-        loads.extend([wt_load, x_loads[3]] + scale_loads[6:8] + [wx_load])
-        loads.extend(x_loads[PACK:] + [(bias[:], b.rearrange("(p t) -> p t", t=PACK))])
+        loads.extend([wt_load, x_loads[3]] + scale_loads[6:8] + [x_loads[PACK], wx_load])
+        loads.extend(x_loads[PACK + 1 :] + [(bias[:], b.rearrange("(p t) -> p t", t=PACK))])
         for dst, src in loads:
             nc.sync.dma_start(dst, src)
 
@@ -309,7 +309,7 @@ def tile_list_biasP_kernel(
         xb0_early = placed([P, 2 * PACK * W], BF16, "xb0_early", 32)
         for t0 in (0, 2):
             weave(woven(xb0_early[:])[:, :, t0 : t0 + 2, :], picked0[:, t0 : t0 + 2, 0 : 2 * W], False)
-        xb0_late = held([P, 2 * PACK * W], BF16, "xb0_late")
+        xb0_late = placed([P, 2 * PACK * W], BF16, "xb0_late", 40)
 
         out_rows = out_0.rearrange("(p t) j -> p t j", t=PACK)
         out_words = out_1[0].rearrange("p j i -> p (j i)").bitcast(I32)

from contextlib import ExitStack

import concourse.mybir as mybir

K, L, N, T, J = 1024, 512, 512, 2048, 1024
FLOPS = 2 * N * J * (K + 2 * L) + 2 * L * L * J

F32 = mybir.dt.float32
BF16 = mybir.dt.bfloat16
I32 = mybir.dt.int32
U32 = mybir.dt.uint32
U16 = mybir.dt.uint16
U8 = mybir.dt.uint8
FP8X4 = mybir.dt.float8_e4m3fn_x4
FP4X4 = mybir.dt.float4_e2m1fn_x4
ALU = mybir.AluOpType
ACT = mybir.ActivationFunctionType

P = 128
PACK = 4
BANK = 512
W = 256
QUARTERS = J // W
SUB = 128
WIDTHS = [W, W, W, SUB, SUB]
STARTS = [sum(WIDTHS[:n]) for n in range(len(WIDTHS))]


def tile_list_biasP_kernel(
    tc, xT, wgt, wt_words, wt_scales, c, wx_words, wx_scales, b, offs, out_0, out_1, out_2
):
    nc = tc.nc
    with ExitStack() as ctx:
        keep = ctx.enter_context(tc.tile_pool(name="keep", bufs=1))
        shared = ctx.enter_context(tc.tile_pool(name="shared", bufs=1))
        psum = ctx.enter_context(tc.psum_pool(name="psum", bufs=8))

        def held(shape, dtype, name):
            return keep.tile(shape, dtype, name=name, align_bytes=64)

        def placed(shape, dtype, name, kib):
            return shared.tile(shape, dtype, name=name, align_bytes=64, offset=kib * 1024)

        def planar(t3):
            return t3.rearrange("p t (q i) -> p q t i", i=4)

        def woven(t2):
            return t2.rearrange("p (q i t) -> p q t i", i=4, t=PACK)

        def weave(out, src, on_vector):
            if on_vector:
                nc.vector.tensor_copy(out=out, in_=planar(src))
            else:
                nc.scalar.activation(out=out, in_=planar(src), func=ACT.Identity)

        def operand(name, width, kib=None):
            codes = held([P, width], U32, name) if kib is None else placed([P, width], U32, name, kib)
            return codes, held([P, width], U8, name + "_scales")

        def quantize(dst, first, src):
            cols = slice(first, first + src.shape[1] // PACK)
            nc.vector.quantize_mx(out=dst[0][:, cols].bitcast(FP8X4), scales=dst[1][:, cols], in_=src)

        offsets = held([P, J // 16], U16, "offsets")
        wt_raw = held([P, 2, 2 * N], U8, "wt_raw")
        wx_raw = placed([P, N], I32, "wx_raw", 40)
        sc_raw = held([P, 2, N], U8, "sc_raw")
        bias = held([P, PACK], F32, "bias")
        wgt_sb = held([P, J], F32, "wgt_sb")
        wgt_rows = held([P, P], F32, "wgt_rows")
        x_sb = [held([P, T], F32, f"x{k}") for k in range(3)] + [placed([P, T], F32, "x3", 48)]
        x_sb.extend(placed([P, T], F32, f"x{PACK + i}", 8 * i) for i in range(PACK))
        c_late = held([P, PACK, 2 * W], F32, "c_late")
        c_sb = [held([P, PACK, W], F32, f"c{h}")[:] for h in range(2)] + [c_late[:, :, 0:W], c_late[:, :, W:]]

        eye = held([P, PACK * (L + 1)], BF16, "eye")
        ones = held([P, P], F32, "ones")
        ramp = held([P, P], F32, "ramp")
        base = held([P, 1], F32, "base")
        turned = held([P, 32], F32, "turned")
        ident = held([P, P], F32, "ident")
        nc.gpsimd.memset(eye[:].bitcast(I32), 0)
        nc.vector.memset(ones[:], 1.0)
        for Q in range(4):
            nc.vector.memset(base[32 * Q : 32 * Q + 32, :], float(32 * Q))
        nc.vector.tensor_tensor_scan(out=ramp[:], data0=ones[:], data1=ones[:], initial=0.0, op0=ALU.mult, op1=ALU.add)
        nc.vector.transpose(out=turned[:], in_=ramp[:, 0:32])
        for out, in0 in (
            (
                eye[:].rearrange("p (t x) -> p t x", t=PACK)[:, :, 0:L:PACK],
                ramp[:].unsqueeze(1).to_broadcast([P, PACK, P]),
            ),
            (ident[:], ramp[:]),
        ):
            nc.vector.tensor_scalar(
                out=out, in0=in0, scalar1=base[:], scalar2=turned[:, 0:1], op0=ALU.subtract, op1=ALU.is_equal
            )
        nc.gpsimd.memset(sc_raw[:].bitcast(I32), 0)
        nc.gpsimd.memset(wgt_rows[64:P, :], 0.0)
        eye_q = operand("eye_q", L)
        quantize(eye_q, 0, eye[:, 0 : PACK * L])

        x_planes = xT.rearrange("(a p i) t -> a i p t", a=2, i=PACK)
        c_rows = c.rearrange("(p t) j -> p t j", t=PACK)
        wt_sc32 = wt_scales.bitcast(I32).rearrange("a q n -> q a n")
        wx_sc32 = wx_scales.bitcast(I32)
        sc32 = sc_raw[:].bitcast(I32)
        scale_loads = []
        for Q in range(4):
            scale_loads.append((sc32[32 * Q : 32 * Q + 4, :, :], wt_sc32[4 * Q : 4 * Q + 4, :, :]))
            scale_loads.append((sc32[32 * Q + 4 : 32 * Q + 8, 0, :], wx_sc32[0, 4 * Q : 4 * Q + 4, :]))
        x_loads = [(x_sb[k][:], x_planes[k // PACK, k % PACK]) for k in range(2 * PACK)]
        wt_load = (wt_raw[:].bitcast(I32), wt_words.bitcast(I32).rearrange("a p n -> p a n"))
        wx_load = (wx_raw[:], wx_words[0].rearrange("p n i -> p (n i)").bitcast(I32))
        loads = [(wgt_rows[0:64, :], wgt[0:P:16, :])]
        loads.extend((c_sb[h], c_rows[:, :, h * W : (h + 1) * W]) for h in range(2))
        loads.extend([(c_late[:], c_rows[:, :, 2 * W :]), (offsets[:], offs), x_loads[0]] + scale_loads[0:2])
        loads.extend([x_loads[1]] + scale_loads[2:4] + [x_loads[2]] + scale_loads[4:6])
        loads.extend([wt_load, x_loads[3]] + scale_loads[6:8] + [x_loads[PACK], wx_load])
        loads.extend(x_loads[PACK + 1 :] + [(bias[:], b.rearrange("(p t) -> p t", t=PACK))])
        for dst, src in loads:
            nc.sync.dma_start(dst, src)

        turned_rows = psum.tile([P, P], F32, name="turned_rows", tag="bank")
        nc.tensor.transpose(turned_rows[:], wgt_rows[:], ident[:])
        spread = [held([P, PACK, 8, 16], F32, f"spread{u}") for u in range(2)]
        for u in range(2):
            blocks = turned_rows[:, 0:64].rearrange("j (g b) -> j b g", b=8)[:, PACK * u : PACK * (u + 1), :]
            nc.scalar.copy(out=spread[u][:], in_=blocks.unsqueeze(3).to_broadcast([P, PACK, 8, 16]))
        wgt_banks = {}

        def turn_wgt(u):
            wgt_banks[u] = psum.tile([P, PACK, P], F32, name="wgt_bank", tag="bank")
            for v in range(PACK):
                nc.tensor.transpose(wgt_banks[u][:, v, :], spread[u][:, v, :, :].rearrange("j g r -> j (g r)"), ident[:])

        def take_wgt(u):
            nc.scalar.copy(out=wgt_sb[:, u * BANK : (u + 1) * BANK], in_=wgt_banks[u][:].rearrange("p v j -> p (v j)"))

        cb = [held([P, PACK * W], BF16, f"cb{h}") for h in range(QUARTERS)]
        cq = [operand(f"cq{h}", W) for h in range(QUARTERS)]
        rb_early = held([P, 2 * PACK * W], BF16, "rb_early")
        rb = [rb_early[:, 0 : PACK * W], rb_early[:, PACK * W :]]
        rb.extend(held([P, PACK * W], BF16, f"rb{h}")[:] for h in (2, 3))

        def round_c(h, pieces, on_vector):
            width = W // pieces
            for j0 in range(0, W, width):
                weave(woven(cb[h][:, PACK * j0 : PACK * (j0 + width)]), c_sb[h][:, :, j0 : j0 + width], on_vector)

        def first_tier(h, pieces):
            width = W // pieces
            for j0 in range(0, W, width):
                quantize(cq[h], j0, cb[h][:, PACK * j0 : PACK * (j0 + width)])

        def decode(h, s):
            cols = slice(s * SUB, (s + 1) * SUB)
            back = psum.tile([P, PACK, SUB], F32, name="back", tag="bank")
            for t in range(PACK):
                nc.tensor.matmul_mx(
                    out=back[:, t, :],
                    lhsT=eye_q[0][:, t * P : (t + 1) * P].bitcast(FP8X4),
                    lhsT_scale=eye_q[1][:, t * P : (t + 1) * P],
                    rhs=cq[h][0][:, cols].bitcast(FP8X4),
                    rhs_scale=cq[h][1][:, cols],
                    start=True,
                    stop=True,
                )
            return back

        def leftover_on_vector(h):
            for s in range(W // SUB):
                back = decode(h, s)
                nc.vector.tensor_tensor(
                    out=woven(rb[h][:, s * PACK * SUB : (s + 1) * PACK * SUB]),
                    in0=planar(c_sb[h][:, :, s * SUB : (s + 1) * SUB]),
                    in1=planar(back[:]),
                    op=ALU.subtract,
                )

        def add_turned(rest, src, first):
            for t in range(PACK):
                nc.tensor.matmul(
                    rest[:, t, :],
                    lhsT=src[:, t, :],
                    rhs=ident[:],
                    is_transpose=True,
                    start=first and t == 0,
                    stop=not first and t == PACK - 1,
                )

        def leftover_in_psum(h):
            pieces = range(W // SUB)
            backs = [decode(h, s) for s in pieces]
            rests = []
            for s in pieces:
                rests.append(psum.tile([P, PACK, P], F32, name="rest", tag="bank"))
                add_turned(rests[s], c_sb[h][:, :, s * SUB : (s + 1) * SUB], True)
            minus = []
            for s in pieces:
                if (h, s) == (QUARTERS - 1, 0):
                    minus.append(placed([P, PACK, SUB], F32, "minus_last", 32))
                else:
                    minus.append(held([P, PACK, SUB], F32, f"minus{h}_{s}"))
                nc.scalar.activation(out=minus[s][:], in_=backs[s][:], func=ACT.Identity, scale=-1.0)
            pairs = []
            for s in pieces:
                add_turned(rests[s], minus[s], False)
                pairs.append(held([P, 2, P, 2], BF16, f"pairs{h}_{s}"))
                nc.scalar.activation(
                    out=pairs[s][:], in_=rests[s][:].rearrange("j (u e) p -> j u p e", e=2), func=ACT.Identity
                )
            words = psum.tile([P, W // SUB, 2, SUB], F32, name="words", tag="bank")
            for s in pieces:
                as_words = pairs[s][:].rearrange("j u p e -> j (u p e)").bitcast(F32)
                for u in range(2):
                    nc.tensor.transpose(words[:, s, u, :], as_words[:, u * P : (u + 1) * P], ident[:])
            nc.scalar.copy(
                out=rb[h].bitcast(F32).rearrange("p (s j u) -> p s j u", s=W // SUB, u=2),
                in_=words[:].rearrange("p s u j -> p s j u"),
            )

        def gather(dst, k, j0, j1):
            nc.vector.tensor_tensor(
                out=dst,
                in0=x_sb[k][:].indirect(offsets[:, j0 // 16 : j1 // 16]),
                in1=wgt_sb[:, j0:j1],
                op=ALU.mult,
            )

        turn_wgt(0)
        turn_wgt(1)
        round_c(0, 2, True)
        round_c(1, 2, False)
        take_wgt(0)
        take_wgt(1)
        first_tier(0, 2)
        first_tier(1, 2)
        leftover_on_vector(0)
        leftover_on_vector(1)
        round_c(2, 1, False)
        round_c(3, 1, False)
        first_tier(2, 1)
        picked0 = held([P, PACK, J], F32, "picked0")
        cr_early = operand("cr_early", 2 * W)
        quantize(cr_early, 0, rb_early[:])
        first_tier(3, 1)
        gather(picked0[:, 0, :], 0, 0, J)
        leftover_in_psum(2)
        leftover_in_psum(3)

        wt_d = held([P, 2 * 2 * N], U8, "wt_d")
        nc.scalar.copy(
            out=wt_d[:].bitcast(U16).rearrange("p (a t q i) -> p a q t i", a=2, t=PACK, i=8),
            in_=wt_raw[:].bitcast(U16).rearrange("p a (q i t) -> p a q t i", t=PACK, i=8),
        )
        wx_d = held([P, N], I32, "wx_d")
        nc.scalar.copy(
            out=wx_d[:].bitcast(U32).rearrange("p (t q i) -> p q t i", t=PACK, i=4),
            in_=wx_raw[:].bitcast(U32).rearrange("p (q i t) -> p q t i", t=PACK, i=4),
        )
        sc_d = held([P, 2 * N], U8, "sc_d")
        nc.vector.tensor_copy(
            out=sc_d[:].rearrange("p (a t q i) -> p a q t i", a=2, t=PACK, i=16),
            in_=sc_raw[:].rearrange("p a (q i t) -> p a q t i", t=PACK, i=16),
        )

        banks = {}

        def sum_of(n, t):
            per_bank = BANK // WIDTHS[n]
            return banks[n, t // per_bank][:, t % per_bank, :]

        def passes(n, weights, moving, first, opens=False, closes=False):
            cols = slice(STARTS[n] - first, STARTS[n] - first + WIDTHS[n])
            per_bank = BANK // WIDTHS[n]
            for t in range(PACK):
                if weights == "wx":
                    lhsT = wx_d[:, t * P : (t + 1) * P].bitcast(FP8X4)
                    lhsT_scale = sc_d[4:P, t * P : (t + 1) * P]
                else:
                    at = weights * N + t * P
                    lhsT = wt_d[:, 2 * at : 2 * (at + P)].bitcast(FP4X4)
                    lhsT_scale = sc_d[:, at : at + P]
                nc.tensor.matmul_mx(
                    out=sum_of(n, t),
                    lhsT=lhsT,
                    lhsT_scale=lhsT_scale,
                    rhs=moving[0][:, cols].bitcast(FP8X4),
                    rhs_scale=moving[1][:, cols],
                    start=opens and t % per_bank == 0,
                    stop=closes and t % per_bank == per_bank - 1,
                )

        def chunks_of(h):
            return [n for n in range(len(WIDTHS)) if STARTS[n] // W == h]

        for n in range(len(WIDTHS)):
            h = STARTS[n] // W
            per_bank = BANK // WIDTHS[n]
            for u in range(PACK // per_bank):
                banks[n, u] = psum.tile([P, per_bank, WIDTHS[n]], F32, name="acc", tag="bank")
            passes(n, "wx", cq[h], h * W, opens=True)
            if h < 2:
                passes(n, "wx", cr_early, 0)

        for k in range(1, PACK):
            gather(picked0[:, k, :], k, 0, J)
        xb0_early = placed([P, 2 * PACK * W], BF16, "xb0_early", 32)
        for t0 in (0, 2):
            weave(woven(xb0_early[:])[:, :, t0 : t0 + 2, :], picked0[:, t0 : t0 + 2, 0 : 2 * W], False)
        xb0_late = placed([P, 2 * PACK * W], BF16, "xb0_late", 40)

        out_rows = out_0.rearrange("(p t) j -> p t j", t=PACK)
        out_words = out_1[0].rearrange("p j i -> p (j i)").bitcast(I32)
        y_scales = held([P, J], U8, "y_scales")
        y = [held([P, PACK, W], F32, f"y{h}") for h in range(QUARTERS)]
        yb = [held([P, PACK * W], BF16, f"yb{h}") for h in range(QUARTERS)]

        stage = held([P, 20 * W], F32, "stage")

        def rows(first, pitch, count, width):
            return stage[:, first * W : (first + count * pitch) * W].rearrange("p (t j) -> p t j", t=count)[:, :, 0:width]

        low_early = rows(0, 10, 2, 2 * W)
        low_third = rows(2, 3, 2, W)
        high = rows(12, 3, 2, 3 * W)
        last = rows(3, 2, PACK, W)
        xb1 = {
            0: stage[:, 4 * W : 6 * W].bitcast(BF16),
            1: placed([P, PACK * W], BF16, "xb1_1", 37)[:],
            2: stage[:, 7 * W + SUB : 9 * W + SUB].bitcast(BF16),
            3: held([P, PACK * W], BF16, "xb1_3")[:],
        }

        def round_pair(h, t0, src, on_vector):
            weave(woven(xb1[h])[:, :, t0 : t0 + 2, :], src, on_vector)

        def close_sums(n):
            h, first = divmod(STARTS[n], W)
            codes = operand(f"xq1_{n}", WIDTHS[n])
            quantize(codes, 0, xb1[h][:, PACK * first : PACK * (first + WIDTHS[n])])
            passes(n, 1, codes, STARTS[n], closes=True)

        def add_bias(h):
            for n in chunks_of(h):
                first = STARTS[n] - h * W
                for t in range(PACK):
                    dst = y[h][:, t, first : first + WIDTHS[n]]
                    nc.scalar.activation(out=dst, in_=sum_of(n, t), func=ACT.Identity, bias=bias[:, t : t + 1])
                    if n == chunks_of(h)[-1] and t % 2 == 1:
                        pair = slice(t - 1, t + 1)
                        nc.sync.dma_start(out_rows[:, pair, h * W : (h + 1) * W], y[h][:, pair, :])

        def round_y(n, on_vector):
            h, first = divmod(STARTS[n], W)
            cols = slice(first, first + WIDTHS[n])
            weave(woven(yb[h][:, PACK * cols.start : PACK * cols.stop]), y[h][:, :, cols], on_vector)

        def hand_on(h):
            cols = slice(h * W, (h + 1) * W)
            y_codes = held([P, W], U32, f"y_codes{h}")
            nc.vector.quantize_mx(out=y_codes[:].bitcast(FP8X4), scales=y_scales[:, cols], in_=yb[h][:])
            nc.sync.dma_start(out_words[:, cols], y_codes[:].bitcast(I32))

        weave(woven(xb0_late[:]), picked0[:, :, 2 * W :], False)
        cr_third = operand("cr_third", W, 48)
        quantize(cr_third, 0, rb[2])
        passes(2, "wx", cr_third, 2 * W)
        gather(stage[:, 0:J], PACK, 0, J)
        gather(low_early[:, 1, :], PACK + 1, 0, 2 * W)
        for h in (0, 1):
            round_pair(h, 0, low_early[:, :, h * W : (h + 1) * W], False)
        xq0_early = operand("xq0_early", 2 * W, 0)
        quantize(xq0_early, 0, xb0_early[:])
        for n in (0, 1):
            passes(n, 0, xq0_early, 0)
        gather(high[:, 0, :], PACK + 2, 0, 3 * W)
        for h in range(3):
            gather(high[:, 1, h * W : (h + 1) * W], PACK + 3, h * W, (h + 1) * W)
        for h in range(3):
            round_pair(h, 2, high[:, :, h * W : (h + 1) * W], False)
        close_sums(0)
        gather(low_third[:, 1, :], PACK + 1, 2 * W, 3 * W)
        close_sums(1)
        round_pair(2, 0, low_third, True)
        xq0_late = operand("xq0_late", 2 * W, 36)
        quantize(xq0_late, 0, xb0_late[:])
        passes(2, 0, xq0_late, 2 * W)
        close_sums(2)
        cr_last = operand("cr_last", W, 38)
        quantize(cr_last, 0, rb[3])
        for n in (3, 4):
            passes(n, 0, xq0_late, 2 * W)
            passes(n, "wx", cr_last, 3 * W)
        add_bias(0)
        add_bias(1)
        round_y(0, False)
        add_bias(2)
        for i in range(1, PACK):
            gather(last[:, i, :], PACK + i, 3 * W, J)
        weave(woven(xb1[3]), last, True)
        close_sums(3)
        close_sums(4)
        round_y(1, False)
        add_bias(3)
        round_y(2, True)
        for h in (0, 2, 1):
            hand_on(h)
        round_y(3, True)
        round_y(4, True)
        hand_on(3)
        for Q in range(4):
            (nc.sync if Q % 2 == 0 else nc.scalar).dma_start(
                out_2[0, 4 * Q : 4 * Q + 4, :].bitcast(I32), y_scales[32 * Q : 32 * Q + 4, :].bitcast(I32)
            )
